import numpy as np
import ml_dtypes


def mxq(x, axis, fmt="e4m3"):
    dtype, down = {"e4m3": (ml_dtypes.float8_e4m3fn, 7), "e5m2": (ml_dtypes.float8_e5m2, 14)}[fmt]
    v = np.moveaxis(np.asarray(x, np.float32).astype(ml_dtypes.bfloat16).astype(np.float64), axis, -1)
    blocks = v.reshape(v.shape[:-1] + (-1, 32))
    amax = np.abs(blocks).max(-1, keepdims=True)
    byte = np.maximum(np.where(amax > 0, np.frexp(amax)[1] - 1 + 127, 0) - down, 1)
    scale = np.exp2(byte - 127.0)
    codes = (blocks / scale).astype(np.float32).astype(dtype).astype(np.float64)
    return np.moveaxis((codes * scale).reshape(v.shape), -1, axis)


WIDE = False


def mx_kscale(k):
    if not WIDE:
        return np.ones(k)
    levels = np.array([10, -10, 5, -5, 0])
    if k % 512:
        return np.exp2(np.random.permutation(np.resize(levels, k // 32))).repeat(32)
    a = np.empty((k // 512, 16))
    for p in range(k // 512):
        a[p, :8] = np.random.permutation(np.resize(levels, 8))
        for g in range(8):
            far = levels[np.abs(levels - a[p, g]) >= 10]
            a[p, g + 8] = far[np.random.randint(len(far))]
    return np.exp2(a.ravel()).repeat(32)


def f64(x):
    return np.asarray(x).astype(np.float64)


def striped(idx):
    return np.tile(idx.reshape(-1, 16).T, (8, 1)).astype(np.uint16)


def unstriped(offs):
    return offs[:16].T.reshape(-1).astype(np.int64)


E2M1 = np.array([0.0, 0.5, 1.0, 1.5, 2.0, 3.0, 4.0, 6.0, -0.0, -0.5, -1.0, -1.5, -2.0, -3.0, -4.0, -6.0])


def pack_weight(w, fmt):
    k, n = w.shape
    w = f64(np.asarray(w, np.float32).astype(ml_dtypes.bfloat16)).reshape(k // 32, 32, n)
    amax = np.abs(w).max(1)
    if fmt == "e4m3":
        byte = np.frexp(amax)[1] - 1 + 127 - 7
    else:
        mant, ex = np.frexp(amax / 6.0)
        byte = np.where(mant > 0.5, ex, ex - 1) + 127
    byte = np.clip(np.where(amax > 0, byte, 1), 1, 254)
    scaled = (w * np.exp2(127.0 - byte)[:, None, :]).reshape(k, n).astype(np.float32)
    by_word = np.ascontiguousarray(scaled.reshape(k // 512, 128, 4, n).transpose(0, 1, 3, 2))
    if fmt == "e4m3":
        words = by_word.astype(ml_dtypes.float8_e4m3fn).view(np.uint8)
    else:
        c = by_word.astype(ml_dtypes.float4_e2m1fn).view(np.uint8) & 0xF
        words = (c[..., 0::2] | (c[..., 1::2] << 4)).reshape(k // 512, 128, 2 * n)
    return np.ascontiguousarray(words), np.ascontiguousarray(byte.astype(np.uint8).reshape(k // 512, 16, n))


def unpack_weight(words, scales, fmt):
    g, _, n = scales.shape
    words = np.ascontiguousarray(words).reshape(g, 128, n, -1)
    if fmt == "e4m3":
        vals = words.view(ml_dtypes.float8_e4m3fn).astype(np.float64)
    else:
        nib = np.empty((g, 128, n, 4), np.uint8)
        nib[..., 0::2] = words & 0xF
        nib[..., 1::2] = words >> 4
        vals = E2M1[nib]
    vals = vals * np.repeat(np.exp2(scales.astype(np.float64) - 127.0), 8, axis=1)[..., None]
    return vals.transpose(0, 1, 3, 2).reshape(g * 512, n)


def silu(v):
    return v / (1.0 + np.exp(-np.maximum(v, -700.0)))


K, T, Q, E, C, D, H = 512, 512, 768, 6, 256, 256, 0
N, TOP = 256, 3


def by_expert(wq, xq, C):
    return np.concatenate([wq[e].T @ xq[:, e * C:(e + 1) * C] for e in range(E)], axis=1)


def setup_inputs():
    n = np.random.standard_normal
    s = mx_kscale(K)
    deal = np.repeat(np.arange(E), C).reshape(TOP, T)[:, np.random.permutation(T)]
    deal = np.take_along_axis(deal, np.argsort(np.random.rand(TOP, T), axis=0), axis=0)
    for _ in range(8):
        s_, t_ = np.random.permutation(T).reshape(2, -1); r = np.random.randint(TOP, size=T // 2); x, y = deal[r, s_].copy(), deal[r, t_].copy()
        ok = ~((deal[:, s_] == y).any(0) | (deal[:, t_] == x).any(0)); deal[r[ok], s_[ok]] = y[ok]; deal[r[ok], t_[ok]] = x[ok]
    order = np.lexsort((np.random.rand(TOP * T), deal.reshape(-1)))
    slot_token = order % T; pos = np.empty(TOP * T, np.int64); pos[order] = np.arange(TOP * T); pos = pos.reshape(TOP, T)
    g = np.random.uniform(0.5, 1.5, (TOP, T)); g = g / g.sum(0)
    slots2 = np.concatenate([np.random.permutation(Q)[:D] for e in range(E)])
    x = pack_weight(n((K, Q)) * s[:, None], "e4m3")
    w = [pack_weight(m, "e2m1") for m in n((E, K, N)) / np.sqrt(K) / s[None, :, None]]
    return {
        "x_words": x[0],
        "x_scales": x[1],
        "xo": (n((K, T)) * s[:, None]).astype(np.float32),
        "w_words": np.stack([m[0] for m in w]),
        "w_scales": np.stack([m[1] for m in w]),
        "gate": np.stack([np.tile(r, (128, 1)) for r in g]).astype(np.float32),
        "offs": striped(slot_token),
        "pos1": striped(pos[0]),
        "pos2": striped(pos[1]),
        "pos3": striped(pos[2]),
        "offs2": striped(slots2),
    }


def reference(x_words, x_scales, xo, w_words, w_scales, gate, offs, pos1, pos2, pos3, offs2):
    w = np.stack([unpack_weight(w_words[e], w_scales[e], "e2m1") for e in range(E)])
    idx, idx2 = unstriped(offs), unstriped(offs2)
    xq = mxq(f64(xo)[:, idx], 0, "e4m3")
    rq = unpack_weight(x_words, x_scales, "e4m3")[:, idx2]
    y = silu(by_expert(w, xq, C))
    z = silu(by_expert(w, rq, D))
    own = sum(f64(gate[r, :1]) * y[:, unstriped(p)] for r, p in enumerate((pos1, pos2, pos3)))
    return np.concatenate([own, z], axis=1)

@@ -1,0 +1,141 @@
+from contextlib import ExitStack
+
+import concourse.mybir as mybir
+
+K, T, Q, E, C, N, TOP = 512, 512, 768, 6, 256, 256, 3
+S = E * C
+P = 128
+FLOPS = 2 * K * N * 2 * S
+BYTES = 4048896
+
+F32 = mybir.dt.float32
+BF16 = mybir.dt.bfloat16
+I32 = mybir.dt.int32
+U32 = mybir.dt.uint32
+U16 = mybir.dt.uint16
+U8 = mybir.dt.uint8
+FP8X4 = mybir.dt.float8_e4m3fn_x4
+FP4X4 = mybir.dt.float4_e2m1fn_x4
+SILU = mybir.ActivationFunctionType.Silu
+MULT = mybir.AluOpType.mult
+ADD = mybir.AluOpType.add
+
+
+def tile_moe_loc_lin_silu_kernel(tc, x_words, x_scales, xo, w_words, w_scales, gate, offs, pos1, pos2, pos3, offs2, out):
+    nc = tc.nc
+    with ExitStack() as ctx:
+        keep = ctx.enter_context(tc.tile_pool(name="keep", bufs=1))
+        ring = ctx.enter_context(tc.tile_pool(name="ring", bufs=3))
+        psum = ctx.enter_context(tc.psum_pool(name="psum", bufs=4))
+
+        def load_list(ap, name):
+            t = keep.tile(list(ap.shape), U16, name=name)
+            nc.sync.dma_start(t[:], ap)
+            return t
+
+        xs = keep.tile([P, Q], U8, name="xs")
+        ws = keep.tile([P, E, N], U8, name="ws", align_bytes=64)
+        nc.vector.memset(xs[:].bitcast(I32), 0)
+        nc.vector.memset(ws[:].bitcast(I32), 0)
+
+        l_offs2 = load_list(offs2, "l_offs2")
+        xw = keep.tile([P, Q], I32, name="xw")
+        nc.sync.dma_start(xw[:], x_words[0].rearrange("p t d -> p (t d)").bitcast(I32))
+        xo_v = xo.rearrange("(p j) t -> p j t", j=4)
+        raw = [keep.tile([P, 2, T], F32, name="raw%d" % u) for u in range(2)]
+        for u in range(2):
+            nc.sync.dma_start(raw[u][:], xo_v[:, 2 * u : 2 * u + 2, :])
+        l_offs = load_list(offs, "l_offs")
+        for r in range(4):
+            nc.sync.dma_start(xs[r:P:32, :].bitcast(I32), x_scales[0][r:16:4, :].bitcast(I32))
+        ww = keep.tile([P, E, 2 * N], U8, name="ww", align_bytes=64)
+        nc.sync.dma_start(ww[:].bitcast(I32), w_words.rearrange("e s p c -> p (e s) c").bitcast(I32))
+        ws_v = w_scales.rearrange("e s b n -> b (e s) n")
+        for r in range(4):
+            nc.sync.dma_start(ws[r:P:32].bitcast(I32), ws_v[r:16:4].bitcast(I32))
+        l_pos = [load_list(p, "l_pos%d" % i) for i, p in enumerate((pos1, pos2, pos3))]
+        g = keep.tile([P, TOP, T], F32, name="g")
+        nc.sync.dma_start(g[:], gate.rearrange("r p t -> p r t"))
+
+        pairs = [keep.tile([P, 2 * T], BF16, name="pairs%d" % u, tag="late%d" % u, align_bytes=64) for u in range(2)]
+        for u in range(2):
+            nc.scalar.copy(pairs[u][:].rearrange("p (t j) -> p t j", j=2), raw[u][:].rearrange("p j t -> p t j"))
+
+        out_v = out.rearrange("(b p) m -> p b m", p=P)
+        y = [keep.tile([P, S], F32, name="y%d" % b) for b in range(2)]
+
+        def products(dst, h, b, operands):
+            bank = psum.tile([P, 2 * C], F32, name="bank")
+            for i in range(2):
+                e = 2 * h + i
+                codes, scales = operands[i]
+                nc.tensor.matmul_mx(
+                    out=bank[:, i * C : (i + 1) * C],
+                    lhsT=ww[:, e, 2 * P * b : 2 * P * (b + 1)].bitcast(FP4X4),
+                    lhsT_scale=ws[:, e, P * b : P * (b + 1)],
+                    rhs=codes.bitcast(FP8X4),
+                    rhs_scale=scales,
+                    start=True,
+                    stop=True,
+                )
+            nc.scalar.activation(dst, bank[:], SILU)
+
+        def their_words(h):
+            rw = keep.tile([P, 2 * C], U32, name="rw%d" % h, align_bytes=64)
+            nc.vector.tensor_copy(rw[:], xw[:].bitcast(U32).indirect(l_offs2[:, 32 * h : 32 * (h + 1)]))
+            return rw
+
+        def their_rest(h, rw, tag):
+            rs = keep.tile([P, 2 * C], U8, name="rs%d" % h, tag=tag, align_bytes=64)
+            nc.vector.tensor_copy(rs[:], xs[:].indirect(l_offs2[:, 32 * h : 32 * (h + 1)]))
+            z = keep.tile([P, 2, 2 * C], F32, name="z%d" % h)
+            ops = [(rw[:, i * C : (i + 1) * C], rs[:, i * C : (i + 1) * C]) for i in range(2)]
+            for b in range(2):
+                products(z[:, b, :], h, b, ops)
+            nc.sync.dma_start(out_v[:, :, T + 2 * C * h : T + 2 * C * (h + 1)], z[:])
+
+        def own_gather(e):
+            got = ring.tile([P, 2, C], U32, name="got")
+            for u in range(2):
+                nc.vector.tensor_copy(got[:, u, :], pairs[u][:].bitcast(U32).indirect(l_offs[:, 16 * e : 16 * (e + 1)]))
+            if e == E - 1:
+                woven = keep.tile([P, 4 * C], BF16, name="woven_last", tag="late2", align_bytes=64)
+            else:
+                woven = ring.tile([P, 4 * C], BF16, name="woven", align_bytes=64)
+            nc.scalar.copy(woven[:].bitcast(U32).rearrange("p (s u) -> p s u", u=2), got[:].rearrange("p u s -> p s u"))
+            return woven
+
+        def own_quantize(e, woven):
+            codes = keep.tile([P, C], U32, name="codes%d" % e, align_bytes=64)
+            scales = keep.tile([P, C], U8, name="scales%d" % e, align_bytes=64)
+            nc.vector.quantize_mx(out=codes[:].bitcast(FP8X4), scales=scales[:], in_=woven[:])
+            return codes[:], scales[:]
+
+        rw = [their_words(h) for h in range(3)]
+        their_rest(0, rw[0], "rs0")
+
+        made = []
+        woven = own_gather(0)
+        for e in range(E):
+            following = own_gather(e + 1) if e + 1 < E else None
+            if e == E - 1:
+                their_rest(1, rw[1], "late1")
+            made.append(own_quantize(e, woven))
+            woven = following
+            if e % 2 == 1:
+                h = e // 2
+                for b in range(2):
+                    products(y[b][:, 2 * C * h : 2 * C * (h + 1)], h, b, made[2 * h : 2 * h + 2])
+        their_rest(2, rw[2], "late2")
+
+        for b in range(2):
+            terms = []
+            for r in range(TOP):
+                term = keep.tile([P, T], F32, name="term%d_%d" % (b, r))
+                nc.vector.tensor_tensor(term[:], y[b][:].indirect(l_pos[r][:]), g[:, r, :], MULT)
+                terms.append(term)
+            part = keep.tile([P, T], F32, name="part%d" % b)
+            nc.vector.tensor_tensor(part[:], terms[0][:], terms[1][:], ADD)
+            own = keep.tile([P, T], F32, name="own%d" % b)
+            nc.vector.tensor_tensor(own[:], part[:], terms[2][:], ADD)
+            nc.sync.dma_start(out_v[:, b, 0:T], own[:])

@@ -1,12 +1,12 @@
 from contextlib import ExitStack
 
 import concourse.mybir as mybir
+from concourse.masks import make_identity
 
 K, T, Q, E, C, N, TOP = 512, 512, 768, 6, 256, 256, 3
 S = E * C
 P = 128
 FLOPS = 2 * K * N * 2 * S
-BYTES = 4048896
 
 F32 = mybir.dt.float32
 BF16 = mybir.dt.bfloat16
@@ -16,6 +16,7 @@ U16 = mybir.dt.uint16
 U8 = mybir.dt.uint8
 FP8X4 = mybir.dt.float8_e4m3fn_x4
 FP4X4 = mybir.dt.float4_e2m1fn_x4
+COPY = mybir.ActivationFunctionType.Copy
 SILU = mybir.ActivationFunctionType.Silu
 MULT = mybir.AluOpType.mult
 ADD = mybir.AluOpType.add
@@ -25,8 +26,10 @@ def tile_moe_loc_lin_silu_kernel(tc, x_words, x_scales, xo, w_words, w_scales, g
     nc = tc.nc
     with ExitStack() as ctx:
         keep = ctx.enter_context(tc.tile_pool(name="keep", bufs=1))
+        two = ctx.enter_context(tc.tile_pool(name="two", bufs=2))
         ring = ctx.enter_context(tc.tile_pool(name="ring", bufs=3))
-        psum = ctx.enter_context(tc.psum_pool(name="psum", bufs=4))
+        late = ctx.enter_context(tc.tile_pool(name="late", bufs=1))
+        psum = ctx.enter_context(tc.psum_pool(name="psum", bufs=1))
 
         def load_list(ap, name):
             t = keep.tile(list(ap.shape), U16, name=name)
@@ -35,44 +38,49 @@ def tile_moe_loc_lin_silu_kernel(tc, x_words, x_scales, xo, w_words, w_scales, g
 
         xs = keep.tile([P, Q], U8, name="xs")
         ws = keep.tile([P, E, N], U8, name="ws", align_bytes=64)
-        nc.vector.memset(xs[:].bitcast(I32), 0)
+        nc.gpsimd.memset(xs[:].bitcast(I32), 0)
         nc.vector.memset(ws[:].bitcast(I32), 0)
+        seed = keep.tile([P, 1], F32, name="seed")
+        nc.gpsimd.memset(seed[:], 0.0)
+        ident = keep.tile([P, P], F32, name="ident")
+        make_identity(nc, ident[:])
 
         l_offs2 = load_list(offs2, "l_offs2")
+        for r in range(4):
+            nc.sync.dma_start(xs[r:P:32, :].bitcast(I32), x_scales[0][r:16:4, :].bitcast(I32))
+        warm = keep.tile([P, 1], F32, name="warm")
+        nc.scalar.activation(warm[:], seed[:], SILU)
         xw = keep.tile([P, Q], I32, name="xw")
         nc.sync.dma_start(xw[:], x_words[0].rearrange("p t d -> p (t d)").bitcast(I32))
         xo_v = xo.rearrange("(p j) t -> p j t", j=4)
-        raw = [keep.tile([P, 2, T], F32, name="raw%d" % u) for u in range(2)]
+        raw = [keep.tile([P, 2, T], F32, name="raw%d" % u, tag="early%d" % u, align_bytes=64) for u in range(2)]
         for u in range(2):
             nc.sync.dma_start(raw[u][:], xo_v[:, 2 * u : 2 * u + 2, :])
         l_offs = load_list(offs, "l_offs")
-        for r in range(4):
-            nc.sync.dma_start(xs[r:P:32, :].bitcast(I32), x_scales[0][r:16:4, :].bitcast(I32))
         ww = keep.tile([P, E, 2 * N], U8, name="ww", align_bytes=64)
         nc.sync.dma_start(ww[:].bitcast(I32), w_words.rearrange("e s p c -> p (e s) c").bitcast(I32))
         ws_v = w_scales.rearrange("e s b n -> b (e s) n")
         for r in range(4):
             nc.sync.dma_start(ws[r:P:32].bitcast(I32), ws_v[r:16:4].bitcast(I32))
         l_pos = [load_list(p, "l_pos%d" % i) for i, p in enumerate((pos1, pos2, pos3))]
-        g = keep.tile([P, TOP, T], F32, name="g")
-        nc.sync.dma_start(g[:], gate.rearrange("r p t -> p r t"))
 
         pairs = [keep.tile([P, 2 * T], BF16, name="pairs%d" % u, tag="late%d" % u, align_bytes=64) for u in range(2)]
         for u in range(2):
             nc.scalar.copy(pairs[u][:].rearrange("p (t j) -> p t j", j=2), raw[u][:].rearrange("p j t -> p t j"))
 
+        grow = keep.tile([P, TOP, T], F32, name="grow", tag="early1", align_bytes=64)
+        nc.sync.dma_start(grow[:], gate.rearrange("r p t -> p r t"))
+
         out_v = out.rearrange("(b p) m -> p b m", p=P)
         y = [keep.tile([P, S], F32, name="y%d" % b) for b in range(2)]
 
-        def products(dst, h, b, operands):
-            bank = psum.tile([P, 2 * C], F32, name="bank")
-            for i in range(2):
-                e = 2 * h + i
-                codes, scales = operands[i]
+        def products(dst, first, b, operands, bank_number):
+            bank = psum.tile([P, len(operands) * C], F32, name="bank", tag="bank%d" % bank_number)
+            for i, (codes, scales) in enumerate(operands):
                 nc.tensor.matmul_mx(
                     out=bank[:, i * C : (i + 1) * C],
-                    lhsT=ww[:, e, 2 * P * b : 2 * P * (b + 1)].bitcast(FP4X4),
-                    lhsT_scale=ws[:, e, P * b : P * (b + 1)],
+                    lhsT=ww[:, first + i, 2 * P * b : 2 * P * (b + 1)].bitcast(FP4X4),
+                    lhsT_scale=ws[:, first + i, P * b : P * (b + 1)],
                     rhs=codes.bitcast(FP8X4),
                     rhs_scale=scales,
                     start=True,
@@ -80,26 +88,27 @@ def tile_moe_loc_lin_silu_kernel(tc, x_words, x_scales, xo, w_words, w_scales, g
                 )
             nc.scalar.activation(dst, bank[:], SILU)
 
-        def their_words(h):
-            rw = keep.tile([P, 2 * C], U32, name="rw%d" % h, align_bytes=64)
-            nc.vector.tensor_copy(rw[:], xw[:].bitcast(U32).indirect(l_offs2[:, 32 * h : 32 * (h + 1)]))
-            return rw
+        def their_words(rw, first):
+            n = rw.shape[1]
+            nc.vector.tensor_copy(rw, xw[:].bitcast(U32).indirect(l_offs2[:, 16 * first : 16 * first + n // 16]))
+            return [rw[:, i : i + C] for i in range(0, n, C)]
 
-        def their_rest(h, rw, tag):
-            rs = keep.tile([P, 2 * C], U8, name="rs%d" % h, tag=tag, align_bytes=64)
-            nc.vector.tensor_copy(rs[:], xs[:].indirect(l_offs2[:, 32 * h : 32 * (h + 1)]))
-            z = keep.tile([P, 2, 2 * C], F32, name="z%d" % h)
-            ops = [(rw[:, i * C : (i + 1) * C], rs[:, i * C : (i + 1) * C]) for i in range(2)]
-            for b in range(2):
-                products(z[:, b, :], h, b, ops)
-            nc.sync.dma_start(out_v[:, :, T + 2 * C * h : T + 2 * C * (h + 1)], z[:])
+        def their_scales(rs, first):
+            n = rs.shape[1]
+            nc.vector.tensor_copy(rs, xs[:].indirect(l_offs2[:, 16 * first : 16 * first + n // 16]))
+            return [rs[:, i : i + C] for i in range(0, n, C)]
+
+        def their_products(h, b):
+            z = keep.tile([P, 2 * C], F32, name="z%d_%d" % (h, b))
+            products(z[:], 2 * h, b, [(rw[e], rs[e]) for e in (2 * h, 2 * h + 1)], 2 + b)
+            nc.sync.dma_start(out_v[:, b, T + 2 * C * h : T + 2 * C * (h + 1)], z[:])
 
         def own_gather(e):
-            got = ring.tile([P, 2, C], U32, name="got")
+            got = two.tile([P, 2, C], U32, name="got")
             for u in range(2):
                 nc.vector.tensor_copy(got[:, u, :], pairs[u][:].bitcast(U32).indirect(l_offs[:, 16 * e : 16 * (e + 1)]))
             if e == E - 1:
-                woven = keep.tile([P, 4 * C], BF16, name="woven_last", tag="late2", align_bytes=64)
+                woven = late.tile([P, 4 * C], BF16, name="woven_last", offset=0, align_bytes=64)
             else:
                 woven = ring.tile([P, 4 * C], BF16, name="woven", align_bytes=64)
             nc.scalar.copy(woven[:].bitcast(U32).rearrange("p (s u) -> p s u", u=2), got[:].rearrange("p u s -> p s u"))
@@ -111,31 +120,75 @@ def tile_moe_loc_lin_silu_kernel(tc, x_words, x_scales, xo, w_words, w_scales, g
             nc.vector.quantize_mx(out=codes[:].bitcast(FP8X4), scales=scales[:], in_=woven[:])
             return codes[:], scales[:]
 
-        rw = [their_words(h) for h in range(3)]
-        their_rest(0, rw[0], "rs0")
+        rs, rw = [], []
+        for h in range(2):
+            bytes_in = keep.tile([P, 2 * C], U8, name="rs%d" % h, align_bytes=64)
+            rs.extend(their_scales(bytes_in[:], 2 * h))
+            words_in = keep.tile([P, 2 * C], U32, name="rw%d" % h, align_bytes=64)
+            rw.extend(their_words(words_in[:], 2 * h))
 
         made = []
         woven = own_gather(0)
         for e in range(E):
             following = own_gather(e + 1) if e + 1 < E else None
             if e == E - 1:
-                their_rest(1, rw[1], "late1")
+                words_in = keep.tile([P, C], U32, name="rw4", tag="late1", align_bytes=64)
+                rw.extend(their_words(words_in[:], E - 2))
             made.append(own_quantize(e, woven))
             woven = following
-            if e % 2 == 1:
-                h = e // 2
+            if e >= E - 2:
                 for b in range(2):
-                    products(y[b][:, 2 * C * h : 2 * C * (h + 1)], h, b, made[2 * h : 2 * h + 2])
-        their_rest(2, rw[2], "late2")
+                    products(y[b][:, C * e : C * (e + 1)], e, b, made[e : e + 1], 2 * (e % 2) + b)
+            elif e % 2 == 1:
+                for b in range(2):
+                    products(y[b][:, C * (e - 1) : C * (e + 1)], e - 1, b, made[e - 1 : e + 1], e - 1 + b)
+        words_in = late.tile([P, C], U32, name="rw5", offset=0, align_bytes=64)
+        rw.extend(their_words(words_in[:], E - 1))
+        bytes_in = late.tile([P, 2 * C], U8, name="rs2", offset=4 * C, align_bytes=64)
+        rs.extend(their_scales(bytes_in[:], E - 2))
+        for h in range(3):
+            for b in range(2):
+                their_products(h, b)
 
-        for b in range(2):
+        def weighted(b, t0, t1):
             terms = []
             for r in range(TOP):
-                term = keep.tile([P, T], F32, name="term%d_%d" % (b, r))
-                nc.vector.tensor_tensor(term[:], y[b][:].indirect(l_pos[r][:]), g[:, r, :], MULT)
+                term = keep.tile([P, t1 - t0], F32, name="term%d_%d_%d" % (b, t0, r))
+                nc.vector.tensor_tensor(term[:], y[b][:].indirect(l_pos[r][:, t0 // 16 : t1 // 16]), grow[:, r, t0:t1], MULT)
                 terms.append(term)
-            part = keep.tile([P, T], F32, name="part%d" % b)
+            return terms
+
+        def sum_on_tensor(b, t0, t1, bank_number):
+            terms = weighted(b, t0, t1)
+            chunks = (t1 - t0) // P
+            turned = psum.tile([P, chunks, P], F32, name="turned", tag="bank%d" % bank_number)
+            for r in range(TOP):
+                for c in range(chunks):
+                    nc.tensor.matmul(
+                        turned[:, c, :],
+                        terms[r][:, c * P : (c + 1) * P],
+                        ident[:],
+                        start=(r == 0 and c == 0),
+                        stop=(r == TOP - 1 and c == chunks - 1),
+                        is_transpose=True,
+                    )
+            sums = keep.tile([P, chunks, P], F32, name="sums%d" % b)
+            nc.scalar.copy(sums[:], turned[:])
+            back = psum.tile([P, chunks, P], F32, name="back", tag="bank%d" % (bank_number + 1))
+            for c in range(chunks):
+                nc.tensor.transpose(back[:, c, :], sums[:, c, :], ident[:])
+            own = keep.tile([P, chunks, P], F32, name="own%d" % b)
+            nc.scalar.copy(own[:], back[:])
+            nc.scalar.dma_start(out_v[:, b, t0:t1], own[:].rearrange("p c t -> p (c t)"))
+
+        def sum_on_vector(b, t0, t1):
+            terms = weighted(b, t0, t1)
+            part = keep.tile([P, t1 - t0], F32, name="part")
             nc.vector.tensor_tensor(part[:], terms[0][:], terms[1][:], ADD)
-            own = keep.tile([P, T], F32, name="own%d" % b)
-            nc.vector.tensor_tensor(own[:], part[:], terms[2][:], ADD)
-            nc.sync.dma_start(out_v[:, b, 0:T], own[:])
+            rest = keep.tile([P, t1 - t0], F32, name="rest")
+            nc.vector.tensor_tensor(rest[:], part[:], terms[2][:], ADD)
+            nc.sync.dma_start(out_v[:, b, t0:t1], rest[:])
+
+        sum_on_tensor(0, 0, T, 4)
+        sum_on_tensor(1, 0, 256, 6)
+        sum_on_vector(1, 256, T)

@@ -121,9 +121,9 @@ def tile_moe_loc_lin_silu_kernel(tc, x_words, x_scales, xo, w_words, w_scales, g
             return codes[:], scales[:]
 
         rs, rw = [], []
+        bytes_in = keep.tile([P, 2 * C], U8, name="rs0", align_bytes=64)
+        rs.extend(their_scales(bytes_in[:], 0))
         for h in range(2):
-            bytes_in = keep.tile([P, 2 * C], U8, name="rs%d" % h, align_bytes=64)
-            rs.extend(their_scales(bytes_in[:], 2 * h))
             words_in = keep.tile([P, 2 * C], U32, name="rw%d" % h, align_bytes=64)
             rw.extend(their_words(words_in[:], 2 * h))
 
@@ -132,20 +132,19 @@ def tile_moe_loc_lin_silu_kernel(tc, x_words, x_scales, xo, w_words, w_scales, g
         for e in range(E):
             following = own_gather(e + 1) if e + 1 < E else None
             if e == E - 1:
-                words_in = keep.tile([P, C], U32, name="rw4", tag="late1", align_bytes=64)
+                words_in = keep.tile([P, 2 * C], U32, name="rw2", tag="late1", align_bytes=64)
                 rw.extend(their_words(words_in[:], E - 2))
             made.append(own_quantize(e, woven))
             woven = following
+            if 1 <= e <= E - 2:
+                first, b = 2 * ((e - 1) // 2), (e - 1) % 2
+                products(y[b][:, C * first : C * (first + 2)], first, b, made[first : first + 2], first + b)
             if e >= E - 2:
                 for b in range(2):
                     products(y[b][:, C * e : C * (e + 1)], e, b, made[e : e + 1], 2 * (e % 2) + b)
-            elif e % 2 == 1:
-                for b in range(2):
-                    products(y[b][:, C * (e - 1) : C * (e + 1)], e - 1, b, made[e - 1 : e + 1], e - 1 + b)
-        words_in = late.tile([P, C], U32, name="rw5", offset=0, align_bytes=64)
-        rw.extend(their_words(words_in[:], E - 1))
-        bytes_in = late.tile([P, 2 * C], U8, name="rs2", offset=4 * C, align_bytes=64)
-        rs.extend(their_scales(bytes_in[:], E - 2))
+        for h in range(1, 3):
+            bytes_in = late.tile([P, 2 * C], U8, name="rs%d" % h, offset=2 * C * h, align_bytes=64)
+            rs.extend(their_scales(bytes_in[:], 2 * h))
         for h in range(3):
             for b in range(2):
                 their_products(h, b)

@@ -26,15 +26,16 @@ def tile_moe_loc_lin_silu_kernel(tc, x_words, x_scales, xo, w_words, w_scales, g
     nc = tc.nc
     with ExitStack() as ctx:
         keep = ctx.enter_context(tc.tile_pool(name="keep", bufs=1))
-        two = ctx.enter_context(tc.tile_pool(name="two", bufs=2))
-        ring = ctx.enter_context(tc.tile_pool(name="ring", bufs=3))
-        late = ctx.enter_context(tc.tile_pool(name="late", bufs=1))
+        laid = ctx.enter_context(tc.tile_pool(name="laid", bufs=1))
         psum = ctx.enter_context(tc.psum_pool(name="psum", bufs=1))
 
         def load_list(ap, name):
             t = keep.tile(list(ap.shape), U16, name=name)
             nc.sync.dma_start(t[:], ap)
             return t
+
+        def placed(shape, dtype, name, offset):
+            return laid.tile(shape, dtype, name=name, offset=offset, align_bytes=64)
 
         xs = keep.tile([P, Q], U8, name="xs")
         ws = keep.tile([P, E, N], U8, name="ws", align_bytes=64)
@@ -47,16 +48,18 @@ def tile_moe_loc_lin_silu_kernel(tc, x_words, x_scales, xo, w_words, w_scales, g
 
         l_offs2 = load_list(offs2, "l_offs2")
         for r in range(4):
-            nc.sync.dma_start(xs[r:P:32, :].bitcast(I32), x_scales[0][r:16:4, :].bitcast(I32))
+            queue = nc.sync if r < 2 else nc.scalar
+            queue.dma_start(xs[r:P:32, :].bitcast(I32), x_scales[0][r:16:4, :].bitcast(I32))
         warm = keep.tile([P, 1], F32, name="warm")
         nc.scalar.activation(warm[:], seed[:], SILU)
+        l_offs = load_list(offs, "l_offs")
+        xo_v = xo.rearrange("(p j) t -> p j t", j=4)
+        raw = keep.tile([P, 4 * T], F32, name="raw", tag="raw", align_bytes=64)
+        for j in range(2):
+            nc.sync.dma_start(raw[:, j * T : (j + 1) * T], xo_v[:, j, :])
         xw = keep.tile([P, Q], I32, name="xw")
         nc.sync.dma_start(xw[:], x_words[0].rearrange("p t d -> p (t d)").bitcast(I32))
-        xo_v = xo.rearrange("(p j) t -> p j t", j=4)
-        raw = [keep.tile([P, 2, T], F32, name="raw%d" % u, tag="early%d" % u, align_bytes=64) for u in range(2)]
-        for u in range(2):
-            nc.sync.dma_start(raw[u][:], xo_v[:, 2 * u : 2 * u + 2, :])
-        l_offs = load_list(offs, "l_offs")
+        nc.sync.dma_start(raw[:, 2 * T :].rearrange("p (j t) -> p j t", j=2), xo_v[:, 2:4, :])
         ww = keep.tile([P, E, 2 * N], U8, name="ww", align_bytes=64)
         nc.sync.dma_start(ww[:].bitcast(I32), w_words.rearrange("e s p c -> p (e s) c").bitcast(I32))
         ws_v = w_scales.rearrange("e s b n -> b (e s) n")
@@ -64,18 +67,15 @@ def tile_moe_loc_lin_silu_kernel(tc, x_words, x_scales, xo, w_words, w_scales, g
             nc.sync.dma_start(ws[r:P:32].bitcast(I32), ws_v[r:16:4].bitcast(I32))
         l_pos = [load_list(p, "l_pos%d" % i) for i, p in enumerate((pos1, pos2, pos3))]
 
-        pairs = [keep.tile([P, 2 * T], BF16, name="pairs%d" % u, tag="late%d" % u, align_bytes=64) for u in range(2)]
-        for u in range(2):
-            nc.scalar.copy(pairs[u][:].rearrange("p (t j) -> p t j", j=2), raw[u][:].rearrange("p j t -> p t j"))
-
-        grow = keep.tile([P, TOP, T], F32, name="grow", tag="early1", align_bytes=64)
-        nc.sync.dma_start(grow[:], gate.rearrange("r p t -> p r t"))
-
         out_v = out.rearrange("(b p) m -> p b m", p=P)
         y = [keep.tile([P, S], F32, name="y%d" % b) for b in range(2)]
+        chunks = T // P
+
+        def bank_tile(number, shape):
+            return psum.tile(shape, F32, name="bank", tag="bank%d" % number)
 
         def products(dst, first, b, operands, bank_number):
-            bank = psum.tile([P, len(operands) * C], F32, name="bank", tag="bank%d" % bank_number)
+            bank = bank_tile(bank_number, [P, len(operands) * C])
             for i, (codes, scales) in enumerate(operands):
                 nc.tensor.matmul_mx(
                     out=bank[:, i * C : (i + 1) * C],
@@ -88,106 +88,151 @@ def tile_moe_loc_lin_silu_kernel(tc, x_words, x_scales, xo, w_words, w_scales, g
                 )
             nc.scalar.activation(dst, bank[:], SILU)
 
-        def their_words(rw, first):
-            n = rw.shape[1]
-            nc.vector.tensor_copy(rw, xw[:].bitcast(U32).indirect(l_offs2[:, 16 * first : 16 * first + n // 16]))
-            return [rw[:, i : i + C] for i in range(0, n, C)]
+        def by_expert(tile):
+            return [tile[:, i : i + C] for i in range(0, tile.shape[1], C)]
 
-        def their_scales(rs, first):
-            n = rs.shape[1]
-            nc.vector.tensor_copy(rs, xs[:].indirect(l_offs2[:, 16 * first : 16 * first + n // 16]))
-            return [rs[:, i : i + C] for i in range(0, n, C)]
+        def their_words(first, count, offset):
+            words = placed([P, count * C], U32, "rw%d" % first, offset)
+            nc.vector.tensor_copy(words[:], xw[:].bitcast(U32).indirect(l_offs2[:, 16 * first : 16 * (first + count)]))
+            rw.extend(by_expert(words))
 
-        def their_products(h, b):
-            z = keep.tile([P, 2 * C], F32, name="z%d_%d" % (h, b))
-            products(z[:], 2 * h, b, [(rw[e], rs[e]) for e in (2 * h, 2 * h + 1)], 2 + b)
-            nc.sync.dma_start(out_v[:, b, T + 2 * C * h : T + 2 * C * (h + 1)], z[:])
+        def their_scales(first, count, offset):
+            scales = placed([P, count * C], U8, "rs%d" % first, offset)
+            nc.vector.tensor_copy(scales[:], xs[:].indirect(l_offs2[:, 16 * first : 16 * (first + count)]))
+            rs.extend(by_expert(scales))
 
-        def own_gather(e):
-            got = two.tile([P, 2, C], U32, name="got")
-            for u in range(2):
-                nc.vector.tensor_copy(got[:, u, :], pairs[u][:].bitcast(U32).indirect(l_offs[:, 16 * e : 16 * (e + 1)]))
-            if e == E - 1:
-                woven = late.tile([P, 4 * C], BF16, name="woven_last", offset=0, align_bytes=64)
-            else:
-                woven = ring.tile([P, 4 * C], BF16, name="woven", align_bytes=64)
-            nc.scalar.copy(woven[:].bitcast(U32).rearrange("p (s u) -> p s u", u=2), got[:].rearrange("p u s -> p s u"))
-            return woven
-
-        def own_quantize(e, woven):
-            codes = keep.tile([P, C], U32, name="codes%d" % e, align_bytes=64)
-            scales = keep.tile([P, C], U8, name="scales%d" % e, align_bytes=64)
-            nc.vector.quantize_mx(out=codes[:].bitcast(FP8X4), scales=scales[:], in_=woven[:])
-            return codes[:], scales[:]
-
-        rs, rw = [], []
-        bytes_in = keep.tile([P, 2 * C], U8, name="rs0", align_bytes=64)
-        rs.extend(their_scales(bytes_in[:], 0))
-        for h in range(2):
-            words_in = keep.tile([P, 2 * C], U32, name="rw%d" % h, align_bytes=64)
-            rw.extend(their_words(words_in[:], 2 * h))
-
-        made = []
-        woven = own_gather(0)
-        for e in range(E):
-            following = own_gather(e + 1) if e + 1 < E else None
-            if e == E - 1:
-                words_in = keep.tile([P, 2 * C], U32, name="rw2", tag="late1", align_bytes=64)
-                rw.extend(their_words(words_in[:], E - 2))
-            made.append(own_quantize(e, woven))
-            woven = following
-            if 1 <= e <= E - 2:
-                first, b = 2 * ((e - 1) // 2), (e - 1) % 2
-                products(y[b][:, C * first : C * (first + 2)], first, b, made[first : first + 2], first + b)
-            if e >= E - 2:
-                for b in range(2):
-                    products(y[b][:, C * e : C * (e + 1)], e, b, made[e : e + 1], 2 * (e % 2) + b)
-        for h in range(1, 3):
-            bytes_in = late.tile([P, 2 * C], U8, name="rs%d" % h, offset=2 * C * h, align_bytes=64)
-            rs.extend(their_scales(bytes_in[:], 2 * h))
-        for h in range(3):
+        def their_products(first, count, bank_number, tags=None):
             for b in range(2):
-                their_products(h, b)
+                name = "z%d_%d" % (first, b)
+                z = keep.tile([P, count * C], F32, name=name, tag=tags[b] if tags else name)
+                products(z[:], first, b, [(rw[e], rs[e]) for e in range(first, first + count)], bank_number + b)
+                (nc.scalar if tags else nc.sync).dma_start(out_v[:, b, T + C * first : T + C * (first + count)], z[:])
 
-        def weighted(b, t0, t1):
-            terms = []
-            for r in range(TOP):
-                term = keep.tile([P, t1 - t0], F32, name="term%d_%d_%d" % (b, t0, r))
-                nc.vector.tensor_tensor(term[:], y[b][:].indirect(l_pos[r][:, t0 // 16 : t1 // 16]), grow[:, r, t0:t1], MULT)
-                terms.append(term)
-            return terms
+        def rows_by_scalar(e, offset):
+            rows = placed([P, 4, C], F32, "rows%d" % e, offset)
+            for j in range(4):
+                nc.scalar.activation(rows[:, j, :], raw[:, j * T : (j + 1) * T].indirect(l_offs[:, 16 * e : 16 * (e + 1)]), COPY)
+            return rows
 
-        def sum_on_tensor(b, t0, t1, bank_number):
-            terms = weighted(b, t0, t1)
-            chunks = (t1 - t0) // P
-            turned = psum.tile([P, chunks, P], F32, name="turned", tag="bank%d" % bank_number)
-            for r in range(TOP):
+        def pairs_by_vector(e, offset):
+            got = placed([P, 2, C], U32, "got%d" % e, offset)
+            for u in range(2):
+                nc.vector.tensor_copy(got[:, u, :], pairs[:].bitcast(U32)[:, u * T :].indirect(l_offs[:, 16 * e : 16 * (e + 1)]))
+            return got
+
+        def weave_rows(dst, rows):
+            nc.gpsimd.tensor_copy(dst.rearrange("p (s j) -> p s j", j=4), rows[:].rearrange("p j s -> p s j"))
+
+        def weave_pairs(move, dst, got):
+            move(dst.bitcast(U32).rearrange("p (s u) -> p s u", u=2), got[:].rearrange("p u s -> p s u"))
+
+        def quantize(first, woven, scales_offset):
+            width = woven.shape[1] // 4
+            codes = keep.tile([P, width], U32, name="codes%d" % first, align_bytes=64)
+            scales = placed([P, width], U8, "scales%d" % first, scales_offset)
+            nc.vector.quantize_mx(out=codes[:].bitcast(FP8X4), scales=scales[:], in_=woven)
+            return list(zip(by_expert(codes), by_expert(scales)))
+
+        def turn(dst, sources):
+            for r, source in enumerate(sources):
                 for c in range(chunks):
                     nc.tensor.matmul(
-                        turned[:, c, :],
-                        terms[r][:, c * P : (c + 1) * P],
+                        dst[:, c, :],
+                        source[:, c * P : (c + 1) * P],
                         ident[:],
                         start=(r == 0 and c == 0),
-                        stop=(r == TOP - 1 and c == chunks - 1),
+                        stop=(r == len(sources) - 1 and c == chunks - 1),
                         is_transpose=True,
                     )
-            sums = keep.tile([P, chunks, P], F32, name="sums%d" % b)
-            nc.scalar.copy(sums[:], turned[:])
-            back = psum.tile([P, chunks, P], F32, name="back", tag="bank%d" % (bank_number + 1))
-            for c in range(chunks):
-                nc.tensor.transpose(back[:, c, :], sums[:, c, :], ident[:])
-            own = keep.tile([P, chunks, P], F32, name="own%d" % b)
-            nc.scalar.copy(own[:], back[:])
-            nc.scalar.dma_start(out_v[:, b, t0:t1], own[:].rearrange("p c t -> p (c t)"))
 
-        def sum_on_vector(b, t0, t1):
-            terms = weighted(b, t0, t1)
-            part = keep.tile([P, t1 - t0], F32, name="part")
-            nc.vector.tensor_tensor(part[:], terms[0][:], terms[1][:], ADD)
-            rest = keep.tile([P, t1 - t0], F32, name="rest")
-            nc.vector.tensor_tensor(rest[:], part[:], terms[2][:], ADD)
-            nc.sync.dma_start(out_v[:, b, t0:t1], rest[:])
+        def gate_columns(r):
+            spread = bank_tile(4 + r, [P, chunks, P])
+            turn(spread, [grow[:, r, :]])
+            nc.scalar.copy(gcol[:, r, :], spread[:, :, 0])
 
-        sum_on_tensor(0, 0, T, 4)
-        sum_on_tensor(1, 0, 256, 6)
-        sum_on_vector(1, 256, T)
+        KB = 1024
+        rs, rw = [], []
+        for h in range(2):
+            their_scales(2 * h, 2, 44 * KB + 512 * h)
+        pairs = keep.tile([P, 4 * T], BF16, name="pairs", align_bytes=64)
+        for u in range(2):
+            nc.gpsimd.tensor_copy(pairs[:, 2 * u * T : 2 * (u + 1) * T].rearrange("p (t j) -> p t j", j=2), raw[:, 2 * u * T : 2 * (u + 1) * T].rearrange("p (j t) -> p t j", j=2))
+        their_words(0, 2, 4 * KB)
+        their_words(2, 2, 9 * KB)
+        rows = {e: rows_by_scalar(e, (12 + 2 * e) * KB) for e in (0, 2)}
+        grow = keep.tile([P, TOP, T], F32, name="grow", tag="raw", align_bytes=64)
+        nc.sync.dma_start(grow[:], gate.rearrange("r p t -> p r t"))
+        got = {e: pairs_by_vector(e, (20 + 2 * e) * KB) for e in (1, 3, 4)}
+        woven = [placed([P, 8 * C], BF16, "woven%d" % h, offset * KB) for h, offset in enumerate((32, 36, 5))]
+
+        def part_of_woven(e):
+            return woven[e // 2][:, 4 * C * (e % 2) : 4 * C * (e % 2 + 1)]
+
+        def own_block(h, b, made):
+            products(y[b][:, 2 * C * h : 2 * C * (h + 1)], 2 * h, b, made, 2 * (h % 2) + b)
+
+        weave_rows(part_of_woven(0), rows[0])
+        weave_rows(part_of_woven(2), rows[2])
+        their_products(0, 2, 4)
+        weave_pairs(nc.scalar.copy, part_of_woven(1), got[1])
+        their_products(2, 2, 6)
+        weave_pairs(nc.gpsimd.tensor_copy, part_of_woven(3), got[3])
+        weave_pairs(nc.gpsimd.tensor_copy, part_of_woven(4), got[4])
+        made = quantize(0, woven[0][:], 40 * KB)
+        got[5] = pairs_by_vector(5, 26 * KB)
+        own_block(0, 0, made)
+        weave_pairs(nc.scalar.copy, part_of_woven(5), got[5])
+        own_block(0, 1, made)
+        gcol = placed([P, 2, chunks], F32, "gcol", 26 * KB)
+        for r in range(2):
+            gate_columns(r)
+        made = quantize(2, woven[1][:], 40 * KB + 512)
+        their_words(4, 1, 28 * KB)
+        for b in range(2):
+            own_block(1, b, made)
+        made = quantize(4, woven[2][:], 41 * KB)
+        for b in range(2):
+            own_block(2, b, made)
+        their_scales(4, 2, 7 * KB)
+        their_words(5, 1, 6 * KB)
+
+        def weighted(b, r, t0, t1):
+            term = keep.tile([P, t1 - t0], F32, name="term%d_%d_%d" % (b, r, t0))
+            nc.vector.tensor_tensor(term[:], y[b][:].indirect(l_pos[r][:, t0 // 16 : t1 // 16]), grow[:, r, t0:t1], MULT)
+            return term
+
+        def fetched(r):
+            plain = keep.tile([P, T], F32, name="plain%d" % r, tag="plain%d" % r)
+            nc.scalar.activation(plain[:], y[1][:].indirect(l_pos[r][:]), COPY)
+            turned = bank_tile(6 + r, [P, chunks, P])
+            turn(turned, [plain])
+            return turned
+
+        def scaled(first, count, bank_number):
+            back = bank_tile(bank_number, [P, count, P])
+            for r in range(2):
+                term = keep.tile([P, count, P], F32, name="scaled%d_%d" % (first, r))
+                for i in range(count):
+                    c = first + i
+                    nc.scalar.activation(term[:, i, :], turned[r][:, c, :], COPY, scale=gcol[:, r, c : c + 1])
+                    nc.tensor.matmul(back[:, i, :], term[:, i, :], ident[:], start=(r == 0 and i == 0), stop=(r == 1 and i == count - 1), is_transpose=True)
+            return back[:].rearrange("p c t -> p (c t)")
+
+        def finish(b, t0, first, second):
+            width = first.shape[1]
+            own = keep.tile([P, width], F32, name="own%d_%d" % (b, t0))
+            nc.vector.tensor_tensor(own[:], first, second, ADD)
+            nc.sync.dma_start(out_v[:, b, t0 : t0 + width], own[:])
+
+        turned = [fetched(r) for r in range(2)]
+        terms = [weighted(0, r, 0, T) for r in range(TOP)]
+        part = keep.tile([P, T], F32, name="part")
+        nc.vector.tensor_tensor(part[:], terms[0][:], terms[1][:], ADD)
+        third_tail = weighted(1, 2, 3 * P, T)
+        finish(0, 0, part[:], terms[2][:])
+        third_head = weighted(1, 2, 0, 3 * P)
+        back = [scaled(0, 2, 4), scaled(2, 1, 5), scaled(3, 1, 0)]
+        their_products(4, 2, 2, ("plain0", "plain1"))
+        finish(1, 0, back[0], third_head[:, : 2 * P])
+        finish(1, 2 * P, back[1], third_head[:, 2 * P :])
+        finish(1, 3 * P, back[2], third_tail[:])

@@ -54,9 +54,8 @@ def tile_moe_loc_lin_silu_kernel(tc, x_words, x_scales, xo, w_words, w_scales, g
         nc.scalar.activation(warm[:], seed[:], SILU)
         l_offs = load_list(offs, "l_offs")
         xo_v = xo.rearrange("(p j) t -> p j t", j=4)
-        raw = keep.tile([P, 4 * T], F32, name="raw", tag="raw", align_bytes=64)
-        for j in range(2):
-            nc.sync.dma_start(raw[:, j * T : (j + 1) * T], xo_v[:, j, :])
+        raw = keep.tile([P, 4 * T], F32, name="raw", align_bytes=64)
+        nc.sync.dma_start(raw[:, : 2 * T].rearrange("p (j t) -> p j t", j=2), xo_v[:, 0:2, :])
         xw = keep.tile([P, Q], I32, name="xw")
         nc.sync.dma_start(xw[:], x_words[0].rearrange("p t d -> p (t d)").bitcast(I32))
         nc.sync.dma_start(raw[:, 2 * T :].rearrange("p (j t) -> p j t", j=2), xo_v[:, 2:4, :])
@@ -66,6 +65,8 @@ def tile_moe_loc_lin_silu_kernel(tc, x_words, x_scales, xo, w_words, w_scales, g
         for r in range(4):
             nc.sync.dma_start(ws[r:P:32].bitcast(I32), ws_v[r:16:4].bitcast(I32))
         l_pos = [load_list(p, "l_pos%d" % i) for i, p in enumerate((pos1, pos2, pos3))]
+        grow = keep.tile([P, TOP, T], F32, name="grow", align_bytes=64)
+        nc.sync.dma_start(grow[:], gate.rearrange("r p t -> p r t"))
 
         out_v = out.rearrange("(b p) m -> p b m", p=P)
         y = [keep.tile([P, S], F32, name="y%d" % b) for b in range(2)]
@@ -123,8 +124,8 @@ def tile_moe_loc_lin_silu_kernel(tc, x_words, x_scales, xo, w_words, w_scales, g
         def weave_rows(dst, rows):
             nc.gpsimd.tensor_copy(dst.rearrange("p (s j) -> p s j", j=4), rows[:].rearrange("p j s -> p s j"))
 
-        def weave_pairs(move, dst, got):
-            move(dst.bitcast(U32).rearrange("p (s u) -> p s u", u=2), got[:].rearrange("p u s -> p s u"))
+        def weave_pairs(dst, got):
+            nc.scalar.copy(dst.bitcast(U32).rearrange("p (s u) -> p s u", u=2), got[:].rearrange("p u s -> p s u"))
 
         def quantize(first, woven, scales_offset):
             width = woven.shape[1] // 4
@@ -160,8 +161,6 @@ def tile_moe_loc_lin_silu_kernel(tc, x_words, x_scales, xo, w_words, w_scales, g
         their_words(0, 2, 4 * KB)
         their_words(2, 2, 9 * KB)
         rows = {e: rows_by_scalar(e, (12 + 2 * e) * KB) for e in (0, 2)}
-        grow = keep.tile([P, TOP, T], F32, name="grow", tag="raw", align_bytes=64)
-        nc.sync.dma_start(grow[:], gate.rearrange("r p t -> p r t"))
         got = {e: pairs_by_vector(e, (20 + 2 * e) * KB) for e in (1, 3, 4)}
         woven = [placed([P, 8 * C], BF16, "woven%d" % h, offset * KB) for h, offset in enumerate((32, 36, 5))]
 
@@ -174,20 +173,20 @@ def tile_moe_loc_lin_silu_kernel(tc, x_words, x_scales, xo, w_words, w_scales, g
         weave_rows(part_of_woven(0), rows[0])
         weave_rows(part_of_woven(2), rows[2])
         their_products(0, 2, 4)
-        weave_pairs(nc.scalar.copy, part_of_woven(1), got[1])
+        weave_pairs(part_of_woven(1), got[1])
         their_products(2, 2, 6)
-        weave_pairs(nc.gpsimd.tensor_copy, part_of_woven(3), got[3])
-        weave_pairs(nc.gpsimd.tensor_copy, part_of_woven(4), got[4])
+        weave_pairs(part_of_woven(3), got[3])
+        weave_pairs(part_of_woven(4), got[4])
         made = quantize(0, woven[0][:], 40 * KB)
-        got[5] = pairs_by_vector(5, 26 * KB)
+        got[5] = pairs_by_vector(5, 16 * KB)
         own_block(0, 0, made)
-        weave_pairs(nc.scalar.copy, part_of_woven(5), got[5])
+        weave_pairs(part_of_woven(5), got[5])
         own_block(0, 1, made)
-        gcol = placed([P, 2, chunks], F32, "gcol", 26 * KB)
+        gcol = placed([P, 2, chunks], F32, "gcol", 16 * KB)
         for r in range(2):
             gate_columns(r)
         made = quantize(2, woven[1][:], 40 * KB + 512)
-        their_words(4, 1, 28 * KB)
+        their_words(4, 1, 36 * KB)
         for b in range(2):
             own_block(1, b, made)
         made = quantize(4, woven[2][:], 41 * KB)

@@ -124,8 +124,8 @@ def tile_moe_loc_lin_silu_kernel(tc, x_words, x_scales, xo, w_words, w_scales, g
         def weave_rows(dst, rows):
             nc.gpsimd.tensor_copy(dst.rearrange("p (s j) -> p s j", j=4), rows[:].rearrange("p j s -> p s j"))
 
-        def weave_pairs(dst, got):
-            nc.scalar.copy(dst.bitcast(U32).rearrange("p (s u) -> p s u", u=2), got[:].rearrange("p u s -> p s u"))
+        def weave_pairs(move, dst, got):
+            move(dst.bitcast(U32).rearrange("p (s u) -> p s u", u=2), got[:].rearrange("p u s -> p s u"))
 
         def quantize(first, woven, scales_offset):
             width = woven.shape[1] // 4
@@ -159,10 +159,10 @@ def tile_moe_loc_lin_silu_kernel(tc, x_words, x_scales, xo, w_words, w_scales, g
         for u in range(2):
             nc.gpsimd.tensor_copy(pairs[:, 2 * u * T : 2 * (u + 1) * T].rearrange("p (t j) -> p t j", j=2), raw[:, 2 * u * T : 2 * (u + 1) * T].rearrange("p (j t) -> p t j", j=2))
         their_words(0, 2, 4 * KB)
-        their_words(2, 2, 9 * KB)
-        rows = {e: rows_by_scalar(e, (12 + 2 * e) * KB) for e in (0, 2)}
+        their_words(2, 2, 48 * KB)
+        rows = {e: rows_by_scalar(e, offset * KB) for e, offset in ((0, 52), (2, 16))}
         got = {e: pairs_by_vector(e, (20 + 2 * e) * KB) for e in (1, 3, 4)}
-        woven = [placed([P, 8 * C], BF16, "woven%d" % h, offset * KB) for h, offset in enumerate((32, 36, 5))]
+        woven = [placed([P, 8 * C], BF16, "woven%d" % h, offset) for h, offset in enumerate((8 * KB + 512, 36 * KB, 5 * KB))]
 
         def part_of_woven(e):
             return woven[e // 2][:, 4 * C * (e % 2) : 4 * C * (e % 2 + 1)]
@@ -173,14 +173,14 @@ def tile_moe_loc_lin_silu_kernel(tc, x_words, x_scales, xo, w_words, w_scales, g
         weave_rows(part_of_woven(0), rows[0])
         weave_rows(part_of_woven(2), rows[2])
         their_products(0, 2, 4)
-        weave_pairs(part_of_woven(1), got[1])
+        weave_pairs(nc.scalar.copy, part_of_woven(1), got[1])
+        weave_pairs(nc.scalar.copy, part_of_woven(3), got[3])
         their_products(2, 2, 6)
-        weave_pairs(part_of_woven(3), got[3])
-        weave_pairs(part_of_woven(4), got[4])
         made = quantize(0, woven[0][:], 40 * KB)
+        weave_pairs(nc.gpsimd.tensor_copy, part_of_woven(4), got[4])
         got[5] = pairs_by_vector(5, 16 * KB)
         own_block(0, 0, made)
-        weave_pairs(part_of_woven(5), got[5])
+        weave_pairs(nc.scalar.copy, part_of_woven(5), got[5])
         own_block(0, 1, made)
         gcol = placed([P, 2, chunks], F32, "gcol", 16 * KB)
         for r in range(2):

@@ -58,7 +58,8 @@ def tile_moe_loc_lin_silu_kernel(tc, x_words, x_scales, xo, w_words, w_scales, g
         nc.sync.dma_start(raw[:, : 2 * T].rearrange("p (j t) -> p j t", j=2), xo_v[:, 0:2, :])
         xw = keep.tile([P, Q], I32, name="xw")
         nc.sync.dma_start(xw[:], x_words[0].rearrange("p t d -> p (t d)").bitcast(I32))
-        nc.sync.dma_start(raw[:, 2 * T :].rearrange("p (j t) -> p j t", j=2), xo_v[:, 2:4, :])
+        for t0 in (0, T // 2):
+            nc.sync.dma_start(raw[:, 2 * T :].rearrange("p (j t) -> p j t", j=2)[:, :, t0 : t0 + T // 2], xo_v[:, 2:4, t0 : t0 + T // 2])
         ww = keep.tile([P, E, 2 * N], U8, name="ww", align_bytes=64)
         nc.sync.dma_start(ww[:].bitcast(I32), w_words.rearrange("e s p c -> p (e s) c").bitcast(I32))
         ws_v = w_scales.rearrange("e s b n -> b (e s) n")
@@ -156,8 +157,11 @@ def tile_moe_loc_lin_silu_kernel(tc, x_words, x_scales, xo, w_words, w_scales, g
         for h in range(2):
             their_scales(2 * h, 2, 44 * KB + 512 * h)
         pairs = keep.tile([P, 4 * T], BF16, name="pairs", align_bytes=64)
-        for u in range(2):
-            nc.gpsimd.tensor_copy(pairs[:, 2 * u * T : 2 * (u + 1) * T].rearrange("p (t j) -> p t j", j=2), raw[:, 2 * u * T : 2 * (u + 1) * T].rearrange("p (j t) -> p t j", j=2))
+        for u, t0, t1 in ((0, 0, T), (1, 0, T // 2), (1, T // 2, T)):
+            nc.gpsimd.tensor_copy(
+                pairs[:, 2 * u * T : 2 * (u + 1) * T].rearrange("p (t j) -> p t j", j=2)[:, t0:t1, :],
+                raw[:, 2 * u * T : 2 * (u + 1) * T].rearrange("p (j t) -> p t j", j=2)[:, t0:t1, :],
+            )
         their_words(0, 2, 4 * KB)
         their_words(2, 2, 48 * KB)
         rows = {e: rows_by_scalar(e, offset * KB) for e, offset in ((0, 52), (2, 16))}

@@ -6,6 +6,7 @@ from concourse.masks import make_identity
 K, T, Q, E, C, N, TOP = 512, 512, 768, 6, 256, 256, 3
 S = E * C
 P = 128
+KB = 1024
 FLOPS = 2 * K * N * 2 * S
 
 F32 = mybir.dt.float32
@@ -39,44 +40,52 @@ def tile_moe_loc_lin_silu_kernel(tc, x_words, x_scales, xo, w_words, w_scales, g
 
         xs = keep.tile([P, Q], U8, name="xs")
         ws = keep.tile([P, E, N], U8, name="ws", align_bytes=64)
-        nc.gpsimd.memset(xs[:].bitcast(I32), 0)
         nc.vector.memset(ws[:].bitcast(I32), 0)
+        plane = keep.tile([P, S], U8, name="plane", align_bytes=64)
+        nc.vector.memset(plane[:].bitcast(I32), 0)
         seed = keep.tile([P, 1], F32, name="seed")
         nc.gpsimd.memset(seed[:], 0.0)
+        chunks = T // P
+        grows = keep.tile([P, P], F32, name="grows")
+        nc.gpsimd.memset(grows[:], 0.0)
         ident = keep.tile([P, P], F32, name="ident")
         make_identity(nc, ident[:])
 
         l_offs2 = load_list(offs2, "l_offs2")
-        for r in range(4):
-            queue = nc.sync if r < 2 else nc.scalar
-            queue.dma_start(xs[r:P:32, :].bitcast(I32), x_scales[0][r:16:4, :].bitcast(I32))
+        nc.scalar.dma_start(xs[:].bitcast(I32), x_scales[0].bitcast(I32).partition_broadcast(P // 16))
         warm = keep.tile([P, 1], F32, name="warm")
         nc.scalar.activation(warm[:], seed[:], SILU)
         l_offs = load_list(offs, "l_offs")
         xo_v = xo.rearrange("(p j) t -> p j t", j=4)
         raw = keep.tile([P, 4 * T], F32, name="raw", align_bytes=64)
-        nc.sync.dma_start(raw[:, : 2 * T].rearrange("p (j t) -> p j t", j=2), xo_v[:, 0:2, :])
-        xw = keep.tile([P, Q], I32, name="xw")
-        nc.sync.dma_start(xw[:], x_words[0].rearrange("p t d -> p (t d)").bitcast(I32))
-        for t0 in (0, T // 2):
-            nc.sync.dma_start(raw[:, 2 * T :].rearrange("p (j t) -> p j t", j=2)[:, :, t0 : t0 + T // 2], xo_v[:, 2:4, t0 : t0 + T // 2])
+        for j in range(4):
+            nc.sync.dma_start(raw[:, j * T : (j + 1) * T], xo_v[:, j, :])
         ww = keep.tile([P, E, 2 * N], U8, name="ww", align_bytes=64)
         nc.sync.dma_start(ww[:].bitcast(I32), w_words.rearrange("e s p c -> p (e s) c").bitcast(I32))
+        xw = keep.tile([P, Q], I32, name="xw")
+        nc.sync.dma_start(xw[:], x_words[0].rearrange("p t d -> p (t d)").bitcast(I32))
+        l_pos = [load_list(p, "l_pos%d" % i) for i, p in enumerate((pos1, pos2, pos3))]
+        grow = [placed([P, T], F32, "grow%d" % r, 2 * r * KB) for r in range(TOP)]
+        for r in range(TOP):
+            nc.sync.dma_start(grow[r][:], gate[r])
+        nc.sync.dma_start(grows[: TOP * chunks, :], gate[:, 0, :].rearrange("r (c t) -> r c t", t=P))
+
         ws_v = w_scales.rearrange("e s b n -> b (e s) n")
         for r in range(4):
             nc.sync.dma_start(ws[r:P:32].bitcast(I32), ws_v[r:16:4].bitcast(I32))
-        l_pos = [load_list(p, "l_pos%d" % i) for i, p in enumerate((pos1, pos2, pos3))]
-        grow = keep.tile([P, TOP, T], F32, name="grow", align_bytes=64)
-        nc.sync.dma_start(grow[:], gate.rearrange("r p t -> p r t"))
+        picked = keep.tile([P, S], U8, name="picked")
+        for h in range(3):
+            nc.vector.tensor_copy(picked[:, 2 * C * h : 2 * C * (h + 1)], xs[:].indirect(l_offs2[:, 32 * h : 32 * (h + 1)]))
+        for q in range(4):
+            nc.sync.dma_start(plane[32 * q : 32 * q + 4, :].bitcast(I32), picked[4 * q : 4 * q + 4, :].bitcast(I32))
 
         out_v = out.rearrange("(b p) m -> p b m", p=P)
-        y = [keep.tile([P, S], F32, name="y%d" % b) for b in range(2)]
-        chunks = T // P
+        y = [placed([P, S], F32, "y%d" % b, (72 + 6 * b) * KB) for b in range(2)]
 
         def bank_tile(number, shape):
             return psum.tile(shape, F32, name="bank", tag="bank%d" % number)
 
-        def products(dst, first, b, operands, bank_number):
+        def multiply(first, b, operands, bank_number):
             bank = bank_tile(bank_number, [P, len(operands) * C])
             for i, (codes, scales) in enumerate(operands):
                 nc.tensor.matmul_mx(
@@ -88,7 +97,7 @@ def tile_moe_loc_lin_silu_kernel(tc, x_words, x_scales, xo, w_words, w_scales, g
                     start=True,
                     stop=True,
                 )
-            nc.scalar.activation(dst, bank[:], SILU)
+            return bank
 
         def by_expert(tile):
             return [tile[:, i : i + C] for i in range(0, tile.shape[1], C)]
@@ -98,144 +107,119 @@ def tile_moe_loc_lin_silu_kernel(tc, x_words, x_scales, xo, w_words, w_scales, g
             nc.vector.tensor_copy(words[:], xw[:].bitcast(U32).indirect(l_offs2[:, 16 * first : 16 * (first + count)]))
             rw.extend(by_expert(words))
 
-        def their_scales(first, count, offset):
-            scales = placed([P, count * C], U8, "rs%d" % first, offset)
-            nc.vector.tensor_copy(scales[:], xs[:].indirect(l_offs2[:, 16 * first : 16 * (first + count)]))
-            rs.extend(by_expert(scales))
 
-        def their_products(first, count, bank_number, tags=None):
-            for b in range(2):
-                name = "z%d_%d" % (first, b)
-                z = keep.tile([P, count * C], F32, name=name, tag=tags[b] if tags else name)
-                products(z[:], first, b, [(rw[e], rs[e]) for e in range(first, first + count)], bank_number + b)
-                (nc.scalar if tags else nc.sync).dma_start(out_v[:, b, T + C * first : T + C * (first + count)], z[:])
+        def their_sums(first, count, banks):
+            return [multiply(first, b, [(rw[e], rs[e]) for e in range(first, first + count)], banks[b]) for b in range(2)]
 
-        def rows_by_scalar(e, offset):
+        def rows_by_scalar(e, width, offset):
             rows = placed([P, 4, C], F32, "rows%d" % e, offset)
             for j in range(4):
-                nc.scalar.activation(rows[:, j, :], raw[:, j * T : (j + 1) * T].indirect(l_offs[:, 16 * e : 16 * (e + 1)]), COPY)
+                nc.scalar.activation(rows[:, j, :], raw[:, j * T : min(j * T + width, 4 * T)].indirect(l_offs[:, 16 * e : 16 * (e + 1)]), COPY)
             return rows
 
-        def pairs_by_vector(e, offset):
-            got = placed([P, 2, C], U32, "got%d" % e, offset)
+        def pairs_by_vector(e):
+            got = placed([P, 2, C], U32, "got%d" % e, (62 + 2 * e if e < 5 else 32) * KB)
             for u in range(2):
-                nc.vector.tensor_copy(got[:, u, :], pairs[:].bitcast(U32)[:, u * T :].indirect(l_offs[:, 16 * e : 16 * (e + 1)]))
+                nc.vector.tensor_copy(got[:, u, :], pairs[u][:].bitcast(U32).indirect(l_offs[:, 16 * e : 16 * (e + 1)]))
             return got
 
         def weave_rows(dst, rows):
             nc.gpsimd.tensor_copy(dst.rearrange("p (s j) -> p s j", j=4), rows[:].rearrange("p j s -> p s j"))
 
-        def weave_pairs(move, dst, got):
-            move(dst.bitcast(U32).rearrange("p (s u) -> p s u", u=2), got[:].rearrange("p u s -> p s u"))
+        def weave_pairs(dst, got):
+            nc.scalar.copy(dst.bitcast(U32).rearrange("p (s u) -> p s u", u=2), got[:].rearrange("p u s -> p s u"))
 
-        def quantize(first, woven, scales_offset):
+        def quantize(first, woven, offset):
             width = woven.shape[1] // 4
-            codes = keep.tile([P, width], U32, name="codes%d" % first, align_bytes=64)
-            scales = placed([P, width], U8, "scales%d" % first, scales_offset)
+            codes = placed([P, width], U32, "codes%d" % first, offset)
+            scales = keep.tile([P, width], U8, name="scales%d" % first, align_bytes=64)
             nc.vector.quantize_mx(out=codes[:].bitcast(FP8X4), scales=scales[:], in_=woven)
             return list(zip(by_expert(codes), by_expert(scales)))
 
-        def turn(dst, sources):
-            for r, source in enumerate(sources):
-                for c in range(chunks):
-                    nc.tensor.matmul(
-                        dst[:, c, :],
-                        source[:, c * P : (c + 1) * P],
-                        ident[:],
-                        start=(r == 0 and c == 0),
-                        stop=(r == len(sources) - 1 and c == chunks - 1),
-                        is_transpose=True,
-                    )
-
-        def gate_columns(r):
-            spread = bank_tile(4 + r, [P, chunks, P])
-            turn(spread, [grow[:, r, :]])
-            nc.scalar.copy(gcol[:, r, :], spread[:, :, 0])
-
-        KB = 1024
-        rs, rw = [], []
-        for h in range(2):
-            their_scales(2 * h, 2, 44 * KB + 512 * h)
-        pairs = keep.tile([P, 4 * T], BF16, name="pairs", align_bytes=64)
-        for u, t0, t1 in ((0, 0, T), (1, 0, T // 2), (1, T // 2, T)):
+        rw = []
+        rs = by_expert(plane)
+        pairs = [keep.tile([P, 2 * T], BF16, name="pairs%d" % u, align_bytes=64) for u in range(2)]
+        for u in range(2):
             nc.gpsimd.tensor_copy(
-                pairs[:, 2 * u * T : 2 * (u + 1) * T].rearrange("p (t j) -> p t j", j=2)[:, t0:t1, :],
-                raw[:, 2 * u * T : 2 * (u + 1) * T].rearrange("p (j t) -> p t j", j=2)[:, t0:t1, :],
+                pairs[u][:].rearrange("p (t j) -> p t j", j=2),
+                raw[:, 2 * u * T : 2 * (u + 1) * T].rearrange("p (j t) -> p t j", j=2),
             )
-        their_words(0, 2, 4 * KB)
-        their_words(2, 2, 48 * KB)
-        rows = {e: rows_by_scalar(e, offset * KB) for e, offset in ((0, 52), (2, 16))}
-        got = {e: pairs_by_vector(e, (20 + 2 * e) * KB) for e in (1, 3, 4)}
-        woven = [placed([P, 8 * C], BF16, "woven%d" % h, offset) for h, offset in enumerate((8 * KB + 512, 36 * KB, 5 * KB))]
+        rows = {0: rows_by_scalar(0, T, 20 * KB), 4: rows_by_scalar(4, 4 * T, 28 * KB)}
+        got = {e: pairs_by_vector(e) for e in (1, 2, 3, 5)}
+        woven = [placed([P, 8 * C], BF16, "woven%d" % h, (8 + 4 * h) * KB) for h in range(3)]
 
         def part_of_woven(e):
             return woven[e // 2][:, 4 * C * (e % 2) : 4 * C * (e % 2 + 1)]
 
-        def own_block(h, b, made):
-            products(y[b][:, 2 * C * h : 2 * C * (h + 1)], 2 * h, b, made, 2 * (h % 2) + b)
+        for e in (0, 4):
+            weave_rows(part_of_woven(e), rows[e])
+        for e in (1, 2, 3, 5):
+            weave_pairs(part_of_woven(e), got[e])
+        made = [quantize(2 * h, woven[h][:], offset * KB) for h, offset in enumerate((24, 20, 26))]
+        for b, h, bank_number in ((0, 0, 0), (1, 0, 3), (0, 1, 1), (1, 1, 5), (0, 2, 2), (1, 2, 4)):
+            nc.scalar.activation(y[b][:, 2 * C * h : 2 * C * (h + 1)], multiply(2 * h, b, made[h], bank_number)[:], SILU)
+        their_words(0, 2, 31 * KB)
+        their_words(2, 2, 16 * KB)
+        their_words(4, 2, 18 * KB)
 
-        weave_rows(part_of_woven(0), rows[0])
-        weave_rows(part_of_woven(2), rows[2])
-        their_products(0, 2, 4)
-        weave_pairs(nc.scalar.copy, part_of_woven(1), got[1])
-        weave_pairs(nc.scalar.copy, part_of_woven(3), got[3])
-        their_products(2, 2, 6)
-        made = quantize(0, woven[0][:], 40 * KB)
-        weave_pairs(nc.gpsimd.tensor_copy, part_of_woven(4), got[4])
-        got[5] = pairs_by_vector(5, 16 * KB)
-        own_block(0, 0, made)
-        weave_pairs(nc.scalar.copy, part_of_woven(5), got[5])
-        own_block(0, 1, made)
-        gcol = placed([P, 2, chunks], F32, "gcol", 16 * KB)
-        for r in range(2):
-            gate_columns(r)
-        made = quantize(2, woven[1][:], 40 * KB + 512)
-        their_words(4, 1, 36 * KB)
-        for b in range(2):
-            own_block(1, b, made)
-        made = quantize(4, woven[2][:], 41 * KB)
-        for b in range(2):
-            own_block(2, b, made)
-        their_scales(4, 2, 7 * KB)
-        their_words(5, 1, 6 * KB)
+        spread = bank_tile(6, [P, P])
+        nc.tensor.transpose(spread[:], grows[:], ident[:])
+        gcol = keep.tile([P, TOP, chunks], F32, name="gcol")
+        nc.scalar.copy(gcol[:].rearrange("p r c -> p (r c)"), spread[:, : TOP * chunks])
 
-        def weighted(b, r, t0, t1):
-            term = keep.tile([P, t1 - t0], F32, name="term%d_%d_%d" % (b, r, t0))
-            nc.vector.tensor_tensor(term[:], y[b][:].indirect(l_pos[r][:, t0 // 16 : t1 // 16]), grow[:, r, t0:t1], MULT)
-            return term
+        terms = {}
+        for r in (2, 1, 0):
+            terms[r] = placed([P, T], F32, "term%d" % r, (56 + 2 * r) * KB)
+            nc.vector.tensor_tensor(terms[r][:], y[0][:].indirect(l_pos[r][:]), grow[r][:], MULT)
 
         def fetched(r):
-            plain = keep.tile([P, T], F32, name="plain%d" % r, tag="plain%d" % r)
-            nc.scalar.activation(plain[:], y[1][:].indirect(l_pos[r][:]), COPY)
-            turned = bank_tile(6 + r, [P, chunks, P])
-            turn(turned, [plain])
+            plain = placed([P, chunks, P], F32, "plain%d" % r, (16, 34)[r - 1] * KB)
+            nc.scalar.activation(plain[:].rearrange("p c t -> p (c t)"), y[1][:].indirect(l_pos[r][:]), COPY)
+            return plain
+
+        def fetched_and_turned(r, bank_number):
+            turned = bank_tile(bank_number, [P, chunks, P])
+            plain = fetched(r)
+            for c in range(chunks):
+                nc.tensor.transpose(turned[:, c, :], plain[:, c, :], ident[:])
             return turned
 
-        def scaled(first, count, bank_number):
-            back = bank_tile(bank_number, [P, count, P])
-            for r in range(2):
-                term = keep.tile([P, count, P], F32, name="scaled%d_%d" % (first, r))
-                for i in range(count):
-                    c = first + i
-                    nc.scalar.activation(term[:, i, :], turned[r][:, c, :], COPY, scale=gcol[:, r, c : c + 1])
-                    nc.tensor.matmul(back[:, i, :], term[:, i, :], ident[:], start=(r == 0 and i == 0), stop=(r == 1 and i == count - 1), is_transpose=True)
-            return back[:].rearrange("p c t -> p (c t)")
+        def scale_and_turn_back(r, turned):
+            scaled = placed([P, chunks, P], F32, "scaled%d" % r, (34 + 2 * r) * KB)
+            for c in range(chunks):
+                nc.scalar.activation(scaled[:, c, :], turned[:, c, :], COPY, scale=gcol[:, r, c : c + 1])
+                nc.tensor.matmul(back[c // 2][:, c % 2, :], scaled[:, c, :], ident[:], start=(r == 1 and c % 2 == 0), stop=(r == 2 and c % 2 == 1), is_transpose=True)
 
-        def finish(b, t0, first, second):
-            width = first.shape[1]
-            own = keep.tile([P, width], F32, name="own%d_%d" % (b, t0))
-            nc.vector.tensor_tensor(own[:], first, second, ADD)
-            nc.sync.dma_start(out_v[:, b, t0 : t0 + width], own[:])
+        def their_result(first, b, bank, offset):
+            z = placed([P, 2 * C], F32, "z%d_%d" % (first, b), offset * KB)
+            nc.scalar.activation(z[:], bank[:], SILU)
+            nc.sync.dma_start(out_v[:, b, T + C * first : T + C * (first + 2)], z[:])
 
-        turned = [fetched(r) for r in range(2)]
-        terms = [weighted(0, r, 0, T) for r in range(TOP)]
+        def first_choice(h, offset):
+            term = placed([P, C], F32, "first%d" % h, offset * KB)
+            nc.vector.tensor_tensor(term[:], y[1][:].indirect(l_pos[0][:, 16 * h : 16 * (h + 1)]), grow[0][:, C * h : C * (h + 1)], MULT)
+            return term
+
         part = keep.tile([P, T], F32, name="part")
-        nc.vector.tensor_tensor(part[:], terms[0][:], terms[1][:], ADD)
-        third_tail = weighted(1, 2, 3 * P, T)
-        finish(0, 0, part[:], terms[2][:])
-        third_head = weighted(1, 2, 0, 3 * P)
-        back = [scaled(0, 2, 4), scaled(2, 1, 5), scaled(3, 1, 0)]
-        their_products(4, 2, 2, ("plain0", "plain1"))
-        finish(1, 0, back[0], third_head[:, : 2 * P])
-        finish(1, 2 * P, back[1], third_head[:, 2 * P :])
-        finish(1, 3 * P, back[2], third_tail[:])
+        nc.vector.tensor_tensor(part[:], terms[2][:], terms[1][:], ADD)
+        first = [first_choice(0, 2)]
+        own0 = keep.tile([P, T], F32, name="own0")
+        nc.vector.tensor_tensor(own0[:], part[:], terms[0][:], ADD)
+        first.append(first_choice(1, 58))
+
+        back = [bank_tile(number, [P, 2, P]) for number in (0, 1)]
+        for first_expert, banks in ((0, (5, 2)), (2, (4, 5))):
+            for b, bank in enumerate(their_sums(first_expert, 2, banks)):
+                their_result(first_expert, b, bank, 44 + 2 * (first_expert + b))
+        sums45 = their_sums(4, 2, (2, 4))
+        turned1 = fetched_and_turned(1, 7)
+        turned2 = fetched_and_turned(2, 6)
+        nc.sync.dma_start(out_v[:, 0, :T], own0[:])
+        scale_and_turn_back(1, turned1)
+        their_result(4, 0, sums45[0], 16)
+        scale_and_turn_back(2, turned2)
+        their_result(4, 1, sums45[1], 34)
+        for h in range(2):
+            own1 = keep.tile([P, C], F32, name="own1_%d" % h)
+            nc.vector.tensor_tensor(own1[:], back[h][:].rearrange("p c t -> p (c t)"), first[h][:], ADD)
+            nc.sync.dma_start(out_v[:, 1, C * h : C * (h + 1)], own1[:])

@@ -40,6 +40,8 @@ def tile_moe_loc_lin_silu_kernel(tc, x_words, x_scales, xo, w_words, w_scales, g
 
         xs = keep.tile([P, Q], U8, name="xs")
         ws = keep.tile([P, E, N], U8, name="ws", align_bytes=64)
+        for first_row, last_row in ((32, 64), (64, P)):
+            nc.gpsimd.memset(xs[first_row:last_row, :].bitcast(I32), 0)
         nc.vector.memset(ws[:].bitcast(I32), 0)
         plane = keep.tile([P, S], U8, name="plane", align_bytes=64)
         nc.vector.memset(plane[:].bitcast(I32), 0)
@@ -52,7 +54,7 @@ def tile_moe_loc_lin_silu_kernel(tc, x_words, x_scales, xo, w_words, w_scales, g
         make_identity(nc, ident[:])
 
         l_offs2 = load_list(offs2, "l_offs2")
-        nc.scalar.dma_start(xs[:].bitcast(I32), x_scales[0].bitcast(I32).partition_broadcast(P // 16))
+        nc.scalar.dma_start(xs[:32, :].bitcast(I32), x_scales[0].bitcast(I32).partition_broadcast(2))
         warm = keep.tile([P, 1], F32, name="warm")
         nc.scalar.activation(warm[:], seed[:], SILU)
         l_offs = load_list(offs, "l_offs")

@@ -38,7 +38,7 @@ def tile_moe_loc_lin_silu_kernel(tc, x_words, x_scales, xo, w_words, w_scales, g
         def placed(shape, dtype, name, offset):
             return laid.tile(shape, dtype, name=name, offset=offset, align_bytes=64)
 
-        xs = keep.tile([P, Q], U8, name="xs")
+        xs = placed([P, Q], U8, "xs", 0)
         ws = keep.tile([P, E, N], U8, name="ws", align_bytes=64)
         for first_row, last_row in ((32, 64), (64, P)):
             nc.gpsimd.memset(xs[first_row:last_row, :].bitcast(I32), 0)
@@ -62,24 +62,23 @@ def tile_moe_loc_lin_silu_kernel(tc, x_words, x_scales, xo, w_words, w_scales, g
         raw = keep.tile([P, 4 * T], F32, name="raw", align_bytes=64)
         for j in range(4):
             nc.sync.dma_start(raw[:, j * T : (j + 1) * T], xo_v[:, j, :])
-        ww = keep.tile([P, E, 2 * N], U8, name="ww", align_bytes=64)
-        nc.sync.dma_start(ww[:].bitcast(I32), w_words.rearrange("e s p c -> p (e s) c").bitcast(I32))
         xw = keep.tile([P, Q], I32, name="xw")
         nc.sync.dma_start(xw[:], x_words[0].rearrange("p t d -> p (t d)").bitcast(I32))
-        l_pos = [load_list(p, "l_pos%d" % i) for i, p in enumerate((pos1, pos2, pos3))]
-        grow = [placed([P, T], F32, "grow%d" % r, 2 * r * KB) for r in range(TOP)]
-        for r in range(TOP):
-            nc.sync.dma_start(grow[r][:], gate[r])
-        nc.sync.dma_start(grows[: TOP * chunks, :], gate[:, 0, :].rearrange("r (c t) -> r c t", t=P))
-
+        ww = keep.tile([P, E, 2 * N], U8, name="ww", align_bytes=64)
+        nc.sync.dma_start(ww[:].bitcast(I32), w_words.rearrange("e s p c -> p (e s) c").bitcast(I32))
         ws_v = w_scales.rearrange("e s b n -> b (e s) n")
         for r in range(4):
             nc.sync.dma_start(ws[r:P:32].bitcast(I32), ws_v[r:16:4].bitcast(I32))
-        picked = keep.tile([P, S], U8, name="picked")
+        l_pos = [load_list(p, "l_pos%d" % i) for i, p in enumerate((pos1, pos2, pos3))]
+        nc.sync.dma_start(grows[: TOP * chunks, :], gate[:, 0, :].rearrange("r (c t) -> r c t", t=P))
+
+        picked = placed([P, S], U8, "picked", 6 * KB)
         for h in range(3):
             nc.vector.tensor_copy(picked[:, 2 * C * h : 2 * C * (h + 1)], xs[:].indirect(l_offs2[:, 32 * h : 32 * (h + 1)]))
         for q in range(4):
             nc.sync.dma_start(plane[32 * q : 32 * q + 4, :].bitcast(I32), picked[4 * q : 4 * q + 4, :].bitcast(I32))
+        grow = placed([P, TOP, T], F32, "grow", 0)
+        nc.sync.dma_start(grow[:], gate.rearrange("r p t -> p r t"))
 
         out_v = out.rearrange("(b p) m -> p b m", p=P)
         y = [placed([P, S], F32, "y%d" % b, (72 + 6 * b) * KB) for b in range(2)]
@@ -87,18 +86,21 @@ def tile_moe_loc_lin_silu_kernel(tc, x_words, x_scales, xo, w_words, w_scales, g
         def bank_tile(number, shape):
             return psum.tile(shape, F32, name="bank", tag="bank%d" % number)
 
+        def product(dst, e, b, codes, scales):
+            nc.tensor.matmul_mx(
+                out=dst,
+                lhsT=ww[:, e, 2 * P * b : 2 * P * (b + 1)].bitcast(FP4X4),
+                lhsT_scale=ws[:, e, P * b : P * (b + 1)],
+                rhs=codes.bitcast(FP8X4),
+                rhs_scale=scales,
+                start=True,
+                stop=True,
+            )
+
         def multiply(first, b, operands, bank_number):
             bank = bank_tile(bank_number, [P, len(operands) * C])
             for i, (codes, scales) in enumerate(operands):
-                nc.tensor.matmul_mx(
-                    out=bank[:, i * C : (i + 1) * C],
-                    lhsT=ww[:, first + i, 2 * P * b : 2 * P * (b + 1)].bitcast(FP4X4),
-                    lhsT_scale=ws[:, first + i, P * b : P * (b + 1)],
-                    rhs=codes.bitcast(FP8X4),
-                    rhs_scale=scales,
-                    start=True,
-                    stop=True,
-                )
+                product(bank[:, i * C : (i + 1) * C], first + i, b, codes, scales)
             return bank
 
         def by_expert(tile):
@@ -119,8 +121,8 @@ def tile_moe_loc_lin_silu_kernel(tc, x_words, x_scales, xo, w_words, w_scales, g
                 nc.scalar.activation(rows[:, j, :], raw[:, j * T : min(j * T + width, 4 * T)].indirect(l_offs[:, 16 * e : 16 * (e + 1)]), COPY)
             return rows
 
-        def pairs_by_vector(e):
-            got = placed([P, 2, C], U32, "got%d" % e, (62 + 2 * e if e < 5 else 32) * KB)
+        def pairs_by_vector(e, offset):
+            got = placed([P, 2, C], U32, "got%d" % e, offset)
             for u in range(2):
                 nc.vector.tensor_copy(got[:, u, :], pairs[u][:].bitcast(U32).indirect(l_offs[:, 16 * e : 16 * (e + 1)]))
             return got
@@ -134,7 +136,7 @@ def tile_moe_loc_lin_silu_kernel(tc, x_words, x_scales, xo, w_words, w_scales, g
         def quantize(first, woven, offset):
             width = woven.shape[1] // 4
             codes = placed([P, width], U32, "codes%d" % first, offset)
-            scales = keep.tile([P, width], U8, name="scales%d" % first, align_bytes=64)
+            scales = placed([P, width], U8, "scales%d" % first, 6 * KB + C * first)
             nc.vector.quantize_mx(out=codes[:].bitcast(FP8X4), scales=scales[:], in_=woven)
             return list(zip(by_expert(codes), by_expert(scales)))
 
@@ -146,23 +148,33 @@ def tile_moe_loc_lin_silu_kernel(tc, x_words, x_scales, xo, w_words, w_scales, g
                 pairs[u][:].rearrange("p (t j) -> p t j", j=2),
                 raw[:, 2 * u * T : 2 * (u + 1) * T].rearrange("p (j t) -> p t j", j=2),
             )
-        rows = {0: rows_by_scalar(0, T, 20 * KB), 4: rows_by_scalar(4, 4 * T, 28 * KB)}
-        got = {e: pairs_by_vector(e) for e in (1, 2, 3, 5)}
-        woven = [placed([P, 8 * C], BF16, "woven%d" % h, (8 + 4 * h) * KB) for h in range(3)]
+        rows = {0: rows_by_scalar(0, T, 20 * KB), 4: rows_by_scalar(4, 4 * T, 26 * KB)}
+        got = {e: pairs_by_vector(e, offset * KB) for e, offset in ((1, 24), (2, 30), (3, 32), (5, 62))}
 
-        def part_of_woven(e):
-            return woven[e // 2][:, 4 * C * (e % 2) : 4 * C * (e % 2 + 1)]
+        def own_products(h, made, banks):
+            for b in range(2):
+                nc.scalar.activation(y[b][:, 2 * C * h : 2 * C * (h + 1)], multiply(2 * h, b, made, banks[b])[:], SILU)
 
+        def their_expert(e, bank_number, offset):
+            bank = bank_tile(bank_number, [P, 2, C])
+            for b in range(2):
+                product(bank[:, b, :], e, b, rw[e], rs[e])
+            z = placed([P, 2, C], F32, "z%d" % e, offset)
+            nc.scalar.activation(z[:], bank[:], SILU)
+            nc.sync.dma_start(out_v[:, :, T + C * e : T + C * (e + 1)], z[:])
+
+        woven = [placed([P, 8 * C], BF16, "woven%d" % h, offset * KB) for h, offset in enumerate((8, 14, 64))]
         for e in (0, 4):
-            weave_rows(part_of_woven(e), rows[e])
+            weave_rows(woven[e // 2][:, : 4 * C], rows[e])
         for e in (1, 2, 3, 5):
-            weave_pairs(part_of_woven(e), got[e])
-        made = [quantize(2 * h, woven[h][:], offset * KB) for h, offset in enumerate((24, 20, 26))]
-        for b, h, bank_number in ((0, 0, 0), (1, 0, 3), (0, 1, 1), (1, 1, 5), (0, 2, 2), (1, 2, 4)):
-            nc.scalar.activation(y[b][:, 2 * C * h : 2 * C * (h + 1)], multiply(2 * h, b, made[h], bank_number)[:], SILU)
-        their_words(0, 2, 31 * KB)
-        their_words(2, 2, 16 * KB)
-        their_words(4, 2, 18 * KB)
+            weave_pairs(woven[e // 2][:, 4 * C * (e % 2) : 4 * C * (e % 2 + 1)], got[e])
+        their_words(0, 1, 24 * KB)
+        their_expert(0, 7, 42 * KB)
+        for h, banks in enumerate(((0, 3), (1, 5), (2, 4))):
+            own_products(h, quantize(2 * h, woven[h][:], (34, 36, 68)[h] * KB), banks)
+        their_words(1, 1, 8 * KB)
+        their_words(2, 2, 14 * KB)
+        their_words(4, 2, 16 * KB)
 
         spread = bank_tile(6, [P, P])
         nc.tensor.transpose(spread[:], grows[:], ident[:])
@@ -172,10 +184,10 @@ def tile_moe_loc_lin_silu_kernel(tc, x_words, x_scales, xo, w_words, w_scales, g
         terms = {}
         for r in (2, 1, 0):
             terms[r] = placed([P, T], F32, "term%d" % r, (56 + 2 * r) * KB)
-            nc.vector.tensor_tensor(terms[r][:], y[0][:].indirect(l_pos[r][:]), grow[r][:], MULT)
+            nc.vector.tensor_tensor(terms[r][:], y[0][:].indirect(l_pos[r][:]), grow[:, r, :], MULT)
 
         def fetched(r):
-            plain = placed([P, chunks, P], F32, "plain%d" % r, (16, 34)[r - 1] * KB)
+            plain = placed([P, chunks, P], F32, "plain%d" % r, (12 + 2 * r) * KB)
             nc.scalar.activation(plain[:].rearrange("p c t -> p (c t)"), y[1][:].indirect(l_pos[r][:]), COPY)
             return plain
 
@@ -187,40 +199,42 @@ def tile_moe_loc_lin_silu_kernel(tc, x_words, x_scales, xo, w_words, w_scales, g
             return turned
 
         def scale_and_turn_back(r, turned):
-            scaled = placed([P, chunks, P], F32, "scaled%d" % r, (34 + 2 * r) * KB)
+            scaled = placed([P, chunks, P], F32, "scaled%d" % r, (50 + 2 * r) * KB)
             for c in range(chunks):
                 nc.scalar.activation(scaled[:, c, :], turned[:, c, :], COPY, scale=gcol[:, r, c : c + 1])
                 nc.tensor.matmul(back[c // 2][:, c % 2, :], scaled[:, c, :], ident[:], start=(r == 1 and c % 2 == 0), stop=(r == 2 and c % 2 == 1), is_transpose=True)
 
-        def their_result(first, b, bank, offset):
-            z = placed([P, 2 * C], F32, "z%d_%d" % (first, b), offset * KB)
+        def their_result(first, b, bank, offset, queue):
+            z = placed([P, 2 * C], F32, "z%d_%d" % (first, b), offset)
             nc.scalar.activation(z[:], bank[:], SILU)
-            nc.sync.dma_start(out_v[:, b, T + C * first : T + C * (first + 2)], z[:])
+            queue.dma_start(out_v[:, b, T + C * first : T + C * (first + 2)], z[:])
 
         def first_choice(h, offset):
             term = placed([P, C], F32, "first%d" % h, offset * KB)
-            nc.vector.tensor_tensor(term[:], y[1][:].indirect(l_pos[0][:, 16 * h : 16 * (h + 1)]), grow[0][:, C * h : C * (h + 1)], MULT)
+            nc.vector.tensor_tensor(term[:], y[1][:].indirect(l_pos[0][:, 16 * h : 16 * (h + 1)]), grow[:, 0, C * h : C * (h + 1)], MULT)
             return term
 
+        halves = [slice(C * h, C * (h + 1)) for h in range(2)]
         part = keep.tile([P, T], F32, name="part")
-        nc.vector.tensor_tensor(part[:], terms[2][:], terms[1][:], ADD)
-        first = [first_choice(0, 2)]
         own0 = keep.tile([P, T], F32, name="own0")
-        nc.vector.tensor_tensor(own0[:], part[:], terms[0][:], ADD)
-        first.append(first_choice(1, 58))
+        for half in halves:
+            nc.vector.tensor_tensor(part[:, half], terms[2][:, half], terms[1][:, half], ADD)
+        for half in halves:
+            nc.vector.tensor_tensor(own0[:, half], part[:, half], terms[0][:, half], ADD)
+        first = [first_choice(h, 58 + h) for h in range(2)]
 
-        back = [bank_tile(number, [P, 2, P]) for number in (0, 1)]
-        for first_expert, banks in ((0, (5, 2)), (2, (4, 5))):
-            for b, bank in enumerate(their_sums(first_expert, 2, banks)):
-                their_result(first_expert, b, bank, 44 + 2 * (first_expert + b))
-        sums45 = their_sums(4, 2, (2, 4))
-        turned1 = fetched_and_turned(1, 7)
-        turned2 = fetched_and_turned(2, 6)
+        their_expert(1, 6, 44 * KB)
+        for b, bank in enumerate(their_sums(2, 2, (0, 3))):
+            their_result(2, b, bank, (46 + 2 * b) * KB, nc.sync)
+        sums45 = their_sums(4, 2, (1, 5))
+        turned1 = fetched_and_turned(1, 2)
+        turned2 = fetched_and_turned(2, 4)
+        back = [bank_tile(number, [P, 2, P]) for number in (7, 6)]
         nc.sync.dma_start(out_v[:, 0, :T], own0[:])
         scale_and_turn_back(1, turned1)
-        their_result(4, 0, sums45[0], 16)
+        their_result(4, 0, sums45[0], 14 * KB, nc.sync)
         scale_and_turn_back(2, turned2)
-        their_result(4, 1, sums45[1], 34)
+        their_result(4, 1, sums45[1], 16 * KB, nc.scalar)
         for h in range(2):
             own1 = keep.tile([P, C], F32, name="own1_%d" % h)
             nc.vector.tensor_tensor(own1[:], back[h][:].rearrange("p c t -> p (c t)"), first[h][:], ADD)

@@ -70,7 +70,7 @@ def tile_moe_loc_lin_silu_kernel(tc, x_words, x_scales, xo, w_words, w_scales, g
         for r in range(4):
             nc.sync.dma_start(ws[r:P:32].bitcast(I32), ws_v[r:16:4].bitcast(I32))
         l_pos = [load_list(p, "l_pos%d" % i) for i, p in enumerate((pos1, pos2, pos3))]
-        nc.sync.dma_start(grows[: TOP * chunks, :], gate[:, 0, :].rearrange("r (c t) -> r c t", t=P))
+        nc.sync.dma_start(grows[: 2 * chunks, :], gate[1:, 0, :].rearrange("r (c t) -> r c t", t=P))
 
         picked = placed([P, S], U8, "picked", 6 * KB)
         for h in range(3):
@@ -178,8 +178,8 @@ def tile_moe_loc_lin_silu_kernel(tc, x_words, x_scales, xo, w_words, w_scales, g
 
         spread = bank_tile(6, [P, P])
         nc.tensor.transpose(spread[:], grows[:], ident[:])
-        gcol = keep.tile([P, TOP, chunks], F32, name="gcol")
-        nc.scalar.copy(gcol[:].rearrange("p r c -> p (r c)"), spread[:, : TOP * chunks])
+        gcol = keep.tile([P, 2, chunks], F32, name="gcol")
+        nc.scalar.copy(gcol[:].rearrange("p r c -> p (r c)"), spread[:, : 2 * chunks])
 
         terms = {}
         for r in (2, 1, 0):
@@ -201,7 +201,7 @@ def tile_moe_loc_lin_silu_kernel(tc, x_words, x_scales, xo, w_words, w_scales, g
         def scale_and_turn_back(r, turned):
             scaled = placed([P, chunks, P], F32, "scaled%d" % r, (50 + 2 * r) * KB)
             for c in range(chunks):
-                nc.scalar.activation(scaled[:, c, :], turned[:, c, :], COPY, scale=gcol[:, r, c : c + 1])
+                nc.scalar.activation(scaled[:, c, :], turned[:, c, :], COPY, scale=gcol[:, r - 1, c : c + 1])
                 nc.tensor.matmul(back[c // 2][:, c % 2, :], scaled[:, c, :], ident[:], start=(r == 1 and c % 2 == 0), stop=(r == 2 and c % 2 == 1), is_transpose=True)
 
         def their_result(first, b, bank, offset, queue):

from contextlib import ExitStack

import concourse.mybir as mybir
from concourse.masks import make_identity

K, T, Q, E, C, N, TOP = 512, 512, 768, 6, 256, 256, 3
S = E * C
P = 128
KB = 1024
FLOPS = 2 * K * N * 2 * S

F32 = mybir.dt.float32
BF16 = mybir.dt.bfloat16
I32 = mybir.dt.int32
U32 = mybir.dt.uint32
U16 = mybir.dt.uint16
U8 = mybir.dt.uint8
FP8X4 = mybir.dt.float8_e4m3fn_x4
FP4X4 = mybir.dt.float4_e2m1fn_x4
COPY = mybir.ActivationFunctionType.Copy
SILU = mybir.ActivationFunctionType.Silu
MULT = mybir.AluOpType.mult
ADD = mybir.AluOpType.add


def tile_moe_loc_lin_silu_kernel(tc, x_words, x_scales, xo, w_words, w_scales, gate, offs, pos1, pos2, pos3, offs2, out):
    nc = tc.nc
    with ExitStack() as ctx:
        keep = ctx.enter_context(tc.tile_pool(name="keep", bufs=1))
        laid = ctx.enter_context(tc.tile_pool(name="laid", bufs=1))
        psum = ctx.enter_context(tc.psum_pool(name="psum", bufs=1))

        def load_list(ap, name):
            t = keep.tile(list(ap.shape), U16, name=name)
            nc.sync.dma_start(t[:], ap)
            return t

        def placed(shape, dtype, name, offset):
            return laid.tile(shape, dtype, name=name, offset=offset, align_bytes=64)

        xs = placed([P, Q], U8, "xs", 0)
        ws = keep.tile([P, E, N], U8, name="ws", align_bytes=64)
        for first_row, last_row in ((32, 64), (64, P)):
            nc.gpsimd.memset(xs[first_row:last_row, :].bitcast(I32), 0)
        nc.vector.memset(ws[:].bitcast(I32), 0)
        plane = keep.tile([P, S], U8, name="plane", align_bytes=64)
        nc.vector.memset(plane[:].bitcast(I32), 0)
        seed = keep.tile([P, 1], F32, name="seed")
        nc.gpsimd.memset(seed[:], 0.0)
        chunks = T // P
        grows = keep.tile([P, P], F32, name="grows")
        nc.gpsimd.memset(grows[:], 0.0)
        ident = keep.tile([P, P], F32, name="ident")
        make_identity(nc, ident[:])

        l_offs2 = load_list(offs2, "l_offs2")
        nc.scalar.dma_start(xs[:32, :].bitcast(I32), x_scales[0].bitcast(I32).partition_broadcast(2))
        warm = keep.tile([P, 1], F32, name="warm")
        nc.scalar.activation(warm[:], seed[:], SILU)
        l_offs = load_list(offs, "l_offs")
        xo_v = xo.rearrange("(p j) t -> p j t", j=4)
        raw = keep.tile([P, 4 * T], F32, name="raw", align_bytes=64)
        for j in range(4):
            nc.sync.dma_start(raw[:, j * T : (j + 1) * T], xo_v[:, j, :])
        xw = keep.tile([P, Q], I32, name="xw")
        nc.sync.dma_start(xw[:], x_words[0].rearrange("p t d -> p (t d)").bitcast(I32))
        ww = keep.tile([P, E, 2 * N], U8, name="ww", align_bytes=64)
        nc.sync.dma_start(ww[:].bitcast(I32), w_words.rearrange("e s p c -> p (e s) c").bitcast(I32))
        ws_v = w_scales.rearrange("e s b n -> b (e s) n")
        for r in range(4):
            nc.sync.dma_start(ws[r:P:32].bitcast(I32), ws_v[r:16:4].bitcast(I32))
        l_pos = [load_list(p, "l_pos%d" % i) for i, p in enumerate((pos1, pos2, pos3))]
        nc.sync.dma_start(grows[: 2 * chunks, :], gate[1:, 0, :].rearrange("r (c t) -> r c t", t=P))

        picked = placed([P, S], U8, "picked", 6 * KB)
        for h in range(3):
            nc.vector.tensor_copy(picked[:, 2 * C * h : 2 * C * (h + 1)], xs[:].indirect(l_offs2[:, 32 * h : 32 * (h + 1)]))
        for q in range(4):
            nc.sync.dma_start(plane[32 * q : 32 * q + 4, :].bitcast(I32), picked[4 * q : 4 * q + 4, :].bitcast(I32))
        grow = placed([P, TOP, T], F32, "grow", 0)
        nc.sync.dma_start(grow[:], gate.rearrange("r p t -> p r t"))

        out_v = out.rearrange("(b p) m -> p b m", p=P)
        y = [placed([P, S], F32, "y%d" % b, (72 + 6 * b) * KB) for b in range(2)]

        def bank_tile(number, shape):
            return psum.tile(shape, F32, name="bank", tag="bank%d" % number)

        def product(dst, e, b, codes, scales):
            nc.tensor.matmul_mx(
                out=dst,
                lhsT=ww[:, e, 2 * P * b : 2 * P * (b + 1)].bitcast(FP4X4),
                lhsT_scale=ws[:, e, P * b : P * (b + 1)],
                rhs=codes.bitcast(FP8X4),
                rhs_scale=scales,
                start=True,
                stop=True,
            )

        def multiply(first, b, operands, bank_number):
            bank = bank_tile(bank_number, [P, len(operands) * C])
            for i, (codes, scales) in enumerate(operands):
                product(bank[:, i * C : (i + 1) * C], first + i, b, codes, scales)
            return bank

        def by_expert(tile):
            return [tile[:, i : i + C] for i in range(0, tile.shape[1], C)]

        def their_words(first, count, offset):
            words = placed([P, count * C], U32, "rw%d" % first, offset)
            nc.vector.tensor_copy(words[:], xw[:].bitcast(U32).indirect(l_offs2[:, 16 * first : 16 * (first + count)]))
            rw.extend(by_expert(words))


        def their_sums(first, count, banks):
            return [multiply(first, b, [(rw[e], rs[e]) for e in range(first, first + count)], banks[b]) for b in range(2)]

        def rows_by_scalar(e, width, offset):
            rows = placed([P, 4, C], F32, "rows%d" % e, offset)
            for j in range(4):
                nc.scalar.activation(rows[:, j, :], raw[:, j * T : min(j * T + width, 4 * T)].indirect(l_offs[:, 16 * e : 16 * (e + 1)]), COPY)
            return rows

        def pairs_by_vector(e, offset):
            got = placed([P, 2, C], U32, "got%d" % e, offset)
            for u in range(2):
                nc.vector.tensor_copy(got[:, u, :], pairs[u][:].bitcast(U32).indirect(l_offs[:, 16 * e : 16 * (e + 1)]))
            return got

        def weave_rows(dst, rows):
            nc.gpsimd.tensor_copy(dst.rearrange("p (s j) -> p s j", j=4), rows[:].rearrange("p j s -> p s j"))

        def weave_pairs(dst, got):
            nc.scalar.copy(dst.bitcast(U32).rearrange("p (s u) -> p s u", u=2), got[:].rearrange("p u s -> p s u"))

        def quantize(first, woven, offset):
            width = woven.shape[1] // 4
            codes = placed([P, width], U32, "codes%d" % first, offset)
            scales = placed([P, width], U8, "scales%d" % first, 6 * KB + C * first)
            nc.vector.quantize_mx(out=codes[:].bitcast(FP8X4), scales=scales[:], in_=woven)
            return list(zip(by_expert(codes), by_expert(scales)))

        rw = []
        rs = by_expert(plane)
        pairs = [keep.tile([P, 2 * T], BF16, name="pairs%d" % u, align_bytes=64) for u in range(2)]
        for u in range(2):
            nc.gpsimd.tensor_copy(
                pairs[u][:].rearrange("p (t j) -> p t j", j=2),
                raw[:, 2 * u * T : 2 * (u + 1) * T].rearrange("p (j t) -> p t j", j=2),
            )
        rows = {0: rows_by_scalar(0, T, 20 * KB), 4: rows_by_scalar(4, 4 * T, 26 * KB)}
        got = {e: pairs_by_vector(e, offset * KB) for e, offset in ((1, 24), (2, 30), (3, 32), (5, 62))}

        def own_products(h, made, banks):
            for b in range(2):
                nc.scalar.activation(y[b][:, 2 * C * h : 2 * C * (h + 1)], multiply(2 * h, b, made, banks[b])[:], SILU)

        def their_expert(e, bank_number, offset):
            bank = bank_tile(bank_number, [P, 2, C])
            for b in range(2):
                product(bank[:, b, :], e, b, rw[e], rs[e])
            z = placed([P, 2, C], F32, "z%d" % e, offset)
            nc.scalar.activation(z[:], bank[:], SILU)
            nc.sync.dma_start(out_v[:, :, T + C * e : T + C * (e + 1)], z[:])

        woven = [placed([P, 8 * C], BF16, "woven%d" % h, offset * KB) for h, offset in enumerate((8, 14, 64))]
        for e in (0, 4):
            weave_rows(woven[e // 2][:, : 4 * C], rows[e])
        for e in (1, 2, 3, 5):
            weave_pairs(woven[e // 2][:, 4 * C * (e % 2) : 4 * C * (e % 2 + 1)], got[e])
        their_words(0, 1, 24 * KB)
        their_expert(0, 7, 42 * KB)
        for h, banks in enumerate(((0, 3), (1, 5), (2, 4))):
            own_products(h, quantize(2 * h, woven[h][:], (34, 36, 68)[h] * KB), banks)
        their_words(1, 1, 8 * KB)
        their_words(2, 2, 14 * KB)
        their_words(4, 2, 16 * KB)

        spread = bank_tile(6, [P, P])
        nc.tensor.transpose(spread[:], grows[:], ident[:])
        gcol = keep.tile([P, 2, chunks], F32, name="gcol")
        nc.scalar.copy(gcol[:].rearrange("p r c -> p (r c)"), spread[:, : 2 * chunks])

        terms = {}
        for r in (2, 1, 0):
            terms[r] = placed([P, T], F32, "term%d" % r, (56 + 2 * r) * KB)
            nc.vector.tensor_tensor(terms[r][:], y[0][:].indirect(l_pos[r][:]), grow[:, r, :], MULT)

        def fetched(r):
            plain = placed([P, chunks, P], F32, "plain%d" % r, (12 + 2 * r) * KB)
            nc.scalar.activation(plain[:].rearrange("p c t -> p (c t)"), y[1][:].indirect(l_pos[r][:]), COPY)
            return plain

        def fetched_and_turned(r, bank_number):
            turned = bank_tile(bank_number, [P, chunks, P])
            plain = fetched(r)
            for c in range(chunks):
                nc.tensor.transpose(turned[:, c, :], plain[:, c, :], ident[:])
            return turned

        def scale_and_turn_back(r, turned):
            scaled = placed([P, chunks, P], F32, "scaled%d" % r, (50 + 2 * r) * KB)
            for c in range(chunks):
                nc.scalar.activation(scaled[:, c, :], turned[:, c, :], COPY, scale=gcol[:, r - 1, c : c + 1])
                nc.tensor.matmul(back[c // 2][:, c % 2, :], scaled[:, c, :], ident[:], start=(r == 1 and c % 2 == 0), stop=(r == 2 and c % 2 == 1), is_transpose=True)

        def their_result(first, b, bank, offset, queue):
            z = placed([P, 2 * C], F32, "z%d_%d" % (first, b), offset)
            nc.scalar.activation(z[:], bank[:], SILU)
            queue.dma_start(out_v[:, b, T + C * first : T + C * (first + 2)], z[:])

        def first_choice(h, offset):
            term = placed([P, C], F32, "first%d" % h, offset * KB)
            nc.vector.tensor_tensor(term[:], y[1][:].indirect(l_pos[0][:, 16 * h : 16 * (h + 1)]), grow[:, 0, C * h : C * (h + 1)], MULT)
            return term

        halves = [slice(C * h, C * (h + 1)) for h in range(2)]
        part = keep.tile([P, T], F32, name="part")
        own0 = keep.tile([P, T], F32, name="own0")
        for half in halves:
            nc.vector.tensor_tensor(part[:, half], terms[2][:, half], terms[1][:, half], ADD)
        for half in halves:
            nc.vector.tensor_tensor(own0[:, half], part[:, half], terms[0][:, half], ADD)
        first = [first_choice(h, 58 + h) for h in range(2)]

        their_expert(1, 6, 44 * KB)
        for b, bank in enumerate(their_sums(2, 2, (0, 3))):
            their_result(2, b, bank, (46 + 2 * b) * KB, nc.sync)
        sums45 = their_sums(4, 2, (1, 5))
        turned1 = fetched_and_turned(1, 2)
        turned2 = fetched_and_turned(2, 4)
        back = [bank_tile(number, [P, 2, P]) for number in (7, 6)]
        nc.sync.dma_start(out_v[:, 0, :T], own0[:])
        scale_and_turn_back(1, turned1)
        their_result(4, 0, sums45[0], 14 * KB, nc.sync)
        scale_and_turn_back(2, turned2)
        their_result(4, 1, sums45[1], 16 * KB, nc.scalar)
        for h in range(2):
            own1 = keep.tile([P, C], F32, name="own1_%d" % h)
            nc.vector.tensor_tensor(own1[:], back[h][:].rearrange("p c t -> p (c t)"), first[h][:], ADD)
            nc.sync.dma_start(out_v[:, 1, C * h : C * (h + 1)], own1[:])
